import numpy as np, ml_dtypes
CORES = [242,247,114,119]
N = 4
BF = ml_dtypes.bfloat16
W, C, M, V, D, Q = 2048, 256, 5, 4, 1, 9
LM = 127
def parts(rng):
    return (rng.integers(0, 256, (N, 8, 16, W)), rng.integers(0, W, (N, 8, 16, C)), rng.integers(0, 256, (N, 8, 16, C)),
            rng.integers(0, 16, (N, 8, 16, 1)), rng.integers(48, 81, (N, 8, 16, 1)))
def pack(x, f, z, w, lm):
    return {"rock": x.reshape(N, 128, W).astype(np.float32).astype(BF), "front": np.ascontiguousarray(f.reshape(N, 128, C)).astype(np.int32),
            "vein": z.reshape(N, 128, C).astype(np.float32).astype(BF), "w": w.reshape(N, 128, 1).astype(np.int32), "lim": lm.reshape(N, 128, 1).astype(np.int32)}
def setup_inputs(rng):
    return pack(*parts(rng))
def setup_inputs_alike(rng):
    x, f, z, w, lm = parts(rng); lm = rng.integers(10, 41, (N, 8, 16, 1)); rec = rng.integers(100, 156, (N, 8, 16, 4))
    x = np.take_along_axis(rec, rng.integers(0, 4, (N, 8, 1, W)), 3)
    far = lm + rng.choice(np.array([-1, 0, 0, 0, 1, 2, 3, 4]), (N, 8, 16, C))
    z = np.take_along_axis(rec, rng.integers(0, 4, (N, 8, 1, C)), 3) + rng.choice(np.array([-1, 1]), (N, 8, 16, C)) * far
    f[:, ::2] = rng.choice(np.array([0, W - 1, W // 2, 3]), (N, 4, 16, C))
    f[:, 1] = f[:, 1][..., rng.integers(0, 4, C)]
    return pack(x, f, z, w, lm)
def setup_inputs_corners(rng):
    x, f, z, w, lm = parts(rng); end = np.array([0, 1, 14, 15]); P = C // 2; h = np.arange(P)
    for a in range(N):
        o = [int(b) for b in rng.permutation(8)]
        for g in range(8):
            v = o[g]
            if v == 0:
                lm[a, g] = 0; w[a, g] = 0
            elif v == 1:
                lm[a, g] = LM; w[a, g] = 15
            elif v in (2, 3, 4):
                x[a, g] = rng.integers(200, 256, (16, W)); z[a, g] = rng.integers(0, 61, (16, C)); lm[a, g] = rng.integers(0, 101, (16, 1))
                s = np.arange(16)[:, None] * (W // 32) + rng.integers(0, W // 32, (16, P)); j = rng.integers(W // 2, W, (16, P))
                if v == 2:
                    k = rng.choice(end, P); l = rng.choice(end, P); k[:16] = np.repeat(end, 4); l[:16] = np.tile(end, 4)
                    s[np.maximum(l, rng.integers(0, 16, P)), h] = s[l, h]
                    j[k, h] = (s[l, h] & -8) + rng.integers(0, 8, P)
                    j[np.maximum(k, rng.integers(0, 16, P)), h] = j[k, h]
                if v == 4:
                    s[:] = W - 1; j[:] = W - 1; s[:, :P // 2] = 0; j[:, :P // 2] = 0
                    s[1:, P // 2:3 * P // 4] = W - 21; j[1:, P // 2:3 * P // 4] = W - 3
                f[a, g][:, 0::2] = s; f[a, g][:, 1::2] = j
            elif v == 5:
                r = rng.integers(64, 192, (16, 1)); x[a, g] = r; lm[a, g] = 0
                off = np.argsort(rng.random((16, C)), axis=0) >= rng.integers(Q - 2, Q + 2, C)[None, :]
                z[a, g] = r + np.where(off, rng.choice(np.array([-40, -4, 4, 40]), (16, C)), 0)
            elif v == 6:
                f[a, g] = (W - 1) * rng.integers(0, 2, (16, C)); w[a, g] = 15 * rng.integers(0, 2, (16, 1)); lm[a, g] = LM * rng.integers(0, 2, (16, 1))
            else:
                w[a, g, 0] = 15; w[a, g, 1] = 1; z[a, g][:, ::2] = 0; z[a, g, 0, ::2] = 136; z[a, g, 1, ::2] = 7; f[a, g][:, ::4] = W - 1
                for i, n, u, m in ((2, W - 3, 2037, 0), (6, W - 15, 2039, 2)):
                    z[a, g, 0, i::8] = 135; z[a, g, 1, i::8] = u - 2025; f[a, g][:, i::8] = n
                    x[a, g][:, (((n * (2 * u + 1)) >> (5 + m)) + n + 613 * m + 37 * np.arange(16)) & (W - 1)] = z[a, g][:, i][:, None]
    return pack(x, f, z, w, lm)
def setup_inputs_ends(rng):
    x, f, z, w, lm = parts(rng)
    x = 255 * np.where(rng.random((N, 8, 1, W)) < 0.4, rng.integers(0, 2, (N, 8, 1, W)), rng.integers(0, 2, (N, 8, 16, W)))
    z = 255 * np.where(rng.random((N, 8, 1, C)) < 0.4, rng.integers(0, 2, (N, 8, 1, C)), rng.integers(0, 2, (N, 8, 16, C)))
    f = (W - 1) * rng.integers(0, 2, f.shape); w = 15 * rng.integers(0, 2, w.shape); lm = LM * rng.integers(0, 2, lm.shape)
    for a, g in ((N - 1, 7), (0, 0)):
        w[a, g] = 15; z[a, g][:, [0, C - 2, C - 1]] = 255; z[a, g][:, [3, C - 3]] = 0
        z[a, g][:, [5, C - 4]] = rng.permutation(np.array([255] * 9 + [26] + [0] * 6))[:, None]
        f[a, g, 15][[0, 3, 5, C - 4, C - 3, C - 2, C - 1]] = W - 1
        for u in ((16 * 15 * 255) & 2047, 0):
            x[a, g][:, ((((W - 1) * (2 * u + 1)) >> (5 + np.arange(M))) + W - 1 + 613 * np.arange(M) + 37 * 15) & (W - 1)] = 0
    return pack(x, f, z, w, lm)
def setup_inputs_full(rng):
    x, f, z, w, lm = parts(rng); P = C // 2; h = np.arange(P); n = W // C
    b = int(rng.integers(0, N)); g = int(rng.integers(0, 8)); rest = [q for q in range(N) if q not in (b, (b - D) % N)]; a = rest[int(rng.integers(0, len(rest)))]
    for q in range(N):
        if q != a:
            x[q, g] = rng.integers(200, 256, (16, W)); z[q, g] = rng.integers(0, 61, (16, C)); lm[q, g] = 0
            f[q, g] = n * rng.permutation(C)[None, :] + rng.integers(0, n, (16, C))
    i = np.array([P - 1, 0, P // 2])[:int(rng.integers(1, 4))]
    f[b, g, 15, 2 * i + 1] = (f[b, g, rng.integers(0, 16, len(i)), 2 * i] & -8) + rng.integers(0, 8, len(i))
    x[a] = rng.integers(200, 256, (8, 16, W)); z[a] = rng.integers(0, 61, (8, 16, C)); lm[a] = rng.integers(80, 121, (8, 16, 1))
    k = rng.integers(0, 16, (8, P)); l = rng.integers(0, 16, (8, P)); gr = np.arange(8)[:, None]; fa = f[a]
    fa[gr, k, 2 * h + 1] = (fa[gr, l, 2 * h] & -8) + rng.integers(0, 8, (8, P))
    o = [int(c) for c in rng.permutation(8)]
    f[a, o[0]] = 0; w[a, o[0]] = 0
    f[a, o[1]] = W - 1; w[a, o[1]] = 0; w[a, o[1], 0] = W >> 9; z[a, o[1], 0] = 32
    return pack(x, f, z, w, lm)
def setup_inputs_spread(rng):
    x = np.minimum((np.exp2(8 * rng.random((N, 8, 1, W))) * rng.random((N, 8, 16, W))).astype(np.int64), 255)
    z = np.minimum((np.exp2(8 * rng.random((N, 8, 1, C))) * rng.random((N, 8, 16, C))).astype(np.int64), 255)
    f = np.minimum((W * rng.random((N, 8, 16, C)) ** 3).astype(np.int64), W - 1)
    return pack(x, f, z, rng.integers(0, 16, (N, 8, 16, 1)), np.minimum((128 * rng.random((N, 8, 16, 1)) ** 2).astype(np.int64), LM))
def check_inputs(d):
    bad = []
    for k, hi in (("rock", 255), ("front", W - 1), ("vein", 255), ("w", 15), ("lim", LM)):
        v = np.asarray(d[k]).astype(np.float64)
        if not (np.min(v) >= 0 and np.max(v) <= hi): bad.append("range of " + k)
        elif np.any(v != np.floor(v)): bad.append("whole numbers in " + k)
    return bad
def reference(rock, front, vein, w, lim):
    x = rock.astype(np.float32).astype(np.int64).reshape(N, 8, 16, W)
    f = front.astype(np.int64).reshape(N, 8, 16, C)
    z = vein.astype(np.float32).astype(np.int64).reshape(N, 8, 16, C)
    wt = w.astype(np.int64).reshape(N, 8, 16, 1); lm = lim.astype(np.int64).reshape(N, 8, 16, 1)
    place = np.arange(16)[:, None]; ci = np.arange(C); met = np.zeros(N, np.int64)
    for t in range(V):
        if t > 0:
            f = np.roll(f, D, axis=0); z = np.roll(z, D, axis=0)
        u = np.add.reduce(wt * z, axis=2) & 2047
        dig = np.add.reduce(z, axis=2) & 15
        top = (lm + (met & 3)[:, None, None, None])[..., None]
        for m in range(M):
            c = (((f * (2 * u[:, :, None, :] + 1)) >> (5 + m)) + f + 613 * m + 37 * place) & (W - 1)
            v = np.take_along_axis(x, c.reshape(N, 8, 1, 16 * C), 3).reshape(N, 8, 16, 16, C)
            dif = np.abs(v - z[:, :, :, None, :])
            score = np.add.reduce(dif, axis=2); near = np.count_nonzero(dif <= top, axis=2)
            if m == 0:
                bs, bc, bn = score, c, near
            else:
                less = score < bs; bs = np.where(less, score, bs); bc = np.where(less, c, bc); bn = np.where(less, near, bn)
        f = np.where(bn >= Q, bc, f)
        sen = ci[((ci >> t) & 1) == 0]; jun = sen + (1 << t)
        fs = f[..., sen]; fj = f[..., jun]
        eq = ((fj[:, :, :, None, :] >> 3) == (fs[:, :, None, :, :] >> 3)).reshape(N, 8, 256, C // 2)
        meet = np.any(eq, axis=2)[:, :, None, :]; first = np.argmax(eq, axis=2)[:, :, None, :]
        k = first >> 4; l = first & 15
        met = np.count_nonzero(meet, axis=(1, 2, 3))
        src = place - l + k
        ns = np.where(meet & (place > l) & (src <= 15), np.take_along_axis(fj, np.minimum(np.maximum(src, 0), 15), 2), fs)
        nj = np.where(meet & (place >= k), (((fj * fs) >> 5) + fj + u[..., jun][:, :, None, :]) & (W - 1), fj)
        f = f.copy(); f[..., sen] = ns; f[..., jun] = nj
        e = np.take_along_axis(f, dig[:, :, None, :], 2)
        old = np.take_along_axis(x, e, 3)
        lo = np.full((N, 8, W), C)
        np.minimum.at(lo, (np.arange(N)[:, None, None], np.arange(8)[None, :, None], e[:, :, 0]), np.broadcast_to(ci, (N, 8, C)))
        zl = np.take_along_axis(z, np.minimum(lo, C - 1)[:, :, None, :], 3)
        x = np.where((lo < C)[:, :, None, :], np.maximum(x - (zl >> 2), 0), x)
        z = (z + old) >> 1
    return {"yx": x.reshape(N, 128, W).astype(np.float32).astype(BF), "yf": f.reshape(N, 128, C).astype(np.float32), "yz": z.reshape(N, 128, C).astype(np.float32).astype(BF)}

@@ -1,0 +1,555 @@
+from concourse.mybir import dt, AluOpType as Op, AxisListType, ActivationFunctionType as Act
+
+NEXT = 1
+CH = [("S", 0, 64), ("V", 64, 128), ("S", 128, 192), ("S", 192, 256)]
+GR = [(0, 128), (128, 256)]
+NV = [b - a for k, a, b in CH if k == "V"][0]
+SUB = 16
+KN = 2956 * 10240 - (1 << 24)
+
+f32, bf, f16, i32, u16 = "float32", "bfloat16", "float16", "int32", "uint16"
+SCRATCH = {
+    "X": ("sbuf", [128, 2304], bf), "fin": ("sbuf", [128, 256], i32), "win": ("sbuf", [128, 1], i32), "lin": ("sbuf", [128, 1], i32),
+    "A": ("sbuf", [128, 20480], bf), "D": ("sbuf", [128, 80 * NV], bf), "NR": ("sbuf", [128, 20480], bf), "Zx": ("sbuf", [128, 16 * NV], bf),
+    "off6": ("sbuf", [128, 1536], u16), "offV": ("sbuf", [128, 5 * NV], u16), "c16": ("sbuf", [128, 1280], f16),
+    "usi": ("sbuf", [128, 512], i32), "u2": ("sbuf", [128, 256], i32), "si": ("sbuf", [128, 256], i32), "oh": ("sbuf", [128, 256], f16),
+    "zq": ("sbuf", [128, 256], f16), "P": ("sbuf", [128, 256], f32), "Q": ("sbuf", [128, 1280], i32), "C": ("sbuf", [128, 1280], i32),
+    "Kn": ("sbuf", [128, 256], f32), "KB": ("sbuf", [128, 256], f32), "EQm": ("sbuf", [128, 1280], bf), "TT": ("sbuf", [128, 1280], bf),
+    "nf": ("sbuf", [128, 256], f32), "K2": ("sbuf", [128, 256], f32), "KI": ("sbuf", [128, 256], i32),
+    "SJ": ("sbuf", [128, 256], f16), "Hh": ("sbuf", [128, 256], f16), "EQ2": ("sbuf", [128, 2048], bf), "MK": ("sbuf", [128, 2048], f16),
+    "PJ": ("sbuf", [128, 2048], f16), "mj": ("sbuf", [128, 128], bf), "w1": ("sbuf", [128, 128], bf), "w0": ("sbuf", [128, 128], bf),
+    "wM": ("sbuf", [128, 128], bf), "ms": ("sbuf", [128, 128], bf), "x16": ("sbuf", [128, 128], f16), "nv": ("sbuf", [128, 128], f16),
+    "nvS": ("sbuf", [128, 128], f16), "JS": ("sbuf", [128, 128], f32), "JQ": ("sbuf", [128, 128], i32), "Jn": ("sbuf", [128, 128], i32),
+    "t1": ("sbuf", [128, 128], f16), "t2": ("sbuf", [128, 128], f16), "metc": ("sbuf", [128, 4], f32),
+    "Fm": ("sbuf", [128, 256], f16), "Er": ("sbuf", [128, 256], f16), "Ouf": ("sbuf", [128, 16], f32), "Ol": ("sbuf", [128, 16], u16),
+    "Y": ("sbuf", [128, 256], bf), "zt": ("sbuf", [128, 256], f16), "R1": ("sbuf", [128, 256], f16), "R2": ("sbuf", [128, 256], bf),
+    "EQW": ("sbuf", [128, 16, 256], bf), "lo": ("sbuf", [128, 256], bf), "LI": ("sbuf", [128, 16], f32), "LO": ("sbuf", [128, 16], f32),
+    "Ls": ("sbuf", [128, 16], u16), "yo": ("sbuf", [128, 256], f32),
+    "one": ("sbuf", [128, 512], bf), "BD": ("sbuf", [128, 128], bf), "BD1": ("sbuf", [128, 128], bf), "I": ("sbuf", [128, 128], bf),
+    "Ineg": ("sbuf", [128, 128], bf), "I32": ("sbuf", [128, 128], bf), "Ihalf": ("sbuf", [128, 128], bf), "q9": ("sbuf", [128, 128], bf),
+    "I5": ("sbuf", [128, 640], bf), "E": ("sbuf", [128, 2048], bf), "ES": ("sbuf", [128, 2048], bf), "B": ("sbuf", [128, 2048], bf),
+    "Q4": ("sbuf", [128, 2048], bf), "W2": ("sbuf", [128, 128], bf), "W32": ("sbuf", [128, 128], bf), "BM": ("sbuf", [128, 128], bf),
+    "BN": ("sbuf", [128, 128], bf), "S15": ("sbuf", [128, 128], bf), "KC": ("sbuf", [128, 128], bf), "MCS": ("sbuf", [128, 480], bf),
+    "MCV": ("sbuf", [128, 480], bf), "RC": ("sbuf", [128, 128], f16), "RM": ("sbuf", [128, 480], f16), "io": ("sbuf", [128, 16], f32),
+    "OH": ("sbuf", [128, 16], f32), "PW": ("sbuf", [128, 48], f32), "PT": ("sbuf", [128, 48], f32), "DMi": ("sbuf", [128, 16, 16], f32),
+    "DM": ("sbuf", [128, 16, 16], bf), "IO": ("sbuf", [128, 16], f32),
+}
+COLS = {}
+for _b, _d, _ns in (("colf", f32, ("kc", "kx", "w2c", "p32", "p33", "p4", "limf", "top", "mets")), ("coli", i32, ("pi", "pk", "meti", "mete"))):
+    SCRATCH[_b] = ("sbuf", [128, len(_ns)], _d)
+    for _i, _n in enumerate(_ns):
+        COLS[_n] = (_b, _i)
+for _t in range(4):
+    SCRATCH["F%d" % _t] = ("sbuf", [128, 256], f16)
+    SCRATCH["Z%d" % _t] = ("sbuf", [128, 256], bf)
+    SCRATCH["Zo%d" % _t] = ("sbuf", [128, 256], bf)
+    for _n, _d in (("UH", f16), ("FI", i32), ("FO", f16)):
+        SCRATCH["%s%d" % (_n, _t)] = ("sbuf", [128, 128 >> _t, 2, 1 << _t], _d)
+BANKS = ["pU", "pR", "pS", "pN", "pA", "pB", "p1", "p2"]
+for _n in BANKS:
+    SCRATCH[_n] = ("psum", [128, 512], f32)
+SEMAPHORES = ["sg", "sv", "ss", "st", "loc"] + ["d%d" % i for i in range(5)] + ["o%s%d" % (c, h) for c in "FZ" for h in range(len(GR))] + \
+    ["r%s%d%d" % (c, t, h) for c in "FZ" for t in (1, 2, 3) for h in range(len(GR))]
+
+CYC, TCYC, GATH, WAKE, WIRE = 1.04e-3, 0.52e-3, 1.56, 0.07, 3.0
+
+
+def rank_program(g, core, T, topo):
+    rank = T.rank_of(core)
+    if rank is None:
+        return
+    nrank = len(T.cores)
+    eng = {"g": g, "v": g.vector, "s": g.scalar, "t": g.tensor, "y": g.sync}
+    semof = {"g": "sg", "v": "sv", "s": "ss", "t": "st"}
+    ops = []
+    hist = {}
+
+    def op(q, fn, outs, ins, cost=0.1, sem=None, inc=1):
+        me, deps = len(ops), {}
+        for accs, wr in ((ins, False), (outs, True)):
+            for acc in accs:
+                for w, lo, hi, i in hist.get(acc[1], ()):
+                    own = ops[i][0] == q
+                    if acc[1] in BANKS:
+                        if not own or (acc[2] < hi and lo < acc[3] and (w or wr)):
+                            deps[i] = deps.get(i, False) or not own
+                    elif acc[2] < hi and lo < acc[3] and (w or wr):
+                        deps[i] = deps.get(i, False) or w or not own
+        ops.append([q, fn, cost, deps, sem or semof[q], inc])
+        for accs, wr in ((ins, False), (outs, True)):
+            for acc in accs:
+                mark(acc[1], acc[2], acc[3], wr, me)
+        return me
+
+    def mark(name, lo, hi, wr, me):
+        h = hist.setdefault(name, [])
+        if wr and name not in BANKS:
+            h[:] = [a for a in h if not (lo <= a[1] and a[2] <= hi)]
+        elif name in BANKS:
+            h[:] = [a for a in h if not (lo <= a[1] and a[2] <= hi and ops[a[3]][0] == ops[me][0] and (wr or not a[0]))]
+        h.append((wr, lo, hi, me))
+
+    def v(name, lo=0, hi=None, st=1, r=128):
+        if name in COLS:
+            name, lo = COLS[name]
+            hi = lo + 1
+        hi = SCRATCH[name][1][1] if hi is None else hi
+        ap = T[name][0:r, lo:hi:st] if st > 1 else T[name][0:r, lo:hi]
+        return (ap, name, lo, hi, (hi - lo + st - 1) // st)
+
+    def v4(base, t, a, b, which=None):
+        name, w = "%s%d" % (base, t), 2 << t
+        ap = T[name][:, a // w:b // w, :, :] if which is None else T[name][:, a // w:b // w, which, :]
+        return (ap, name, a, b, b - a if which is None else (b - a) // 2)
+
+    def vcost(o, *ins):
+        two = all(x[1] not in BANKS and SCRATCH[x[1]][2] in (bf, f16, u16) for x in (o,) + ins[:1])
+        if len(ins) == 2:
+            return max(64, o[4] * (1 if ins[0][1] in BANKS or ins[1][1] in BANKS else 2)) * CYC
+        return max(64, o[4] * (0.5 if two else 1)) * CYC
+
+    def tt(o, a, b, f):
+        op("v", lambda: g.vector.tensor_tensor(o[0], a[0], b[0], f), [o], [a, b], vcost(o, a, b))
+
+    def ts(o, a, s1, f1, s2=None, f2=None):
+        ins = [a] + [s for s in (s1, s2) if isinstance(s, tuple)]
+        x1 = s1[0] if isinstance(s1, tuple) else s1
+        x2 = s2[0] if isinstance(s2, tuple) else s2
+        if f2 is None:
+            op("v", lambda: g.vector.tensor_scalar(o[0], a[0], x1, None, f1), [o], ins, vcost(o, a))
+        else:
+            op("v", lambda: g.vector.tensor_scalar(o[0], a[0], x1, x2, f1, f2), [o], ins, vcost(o, a))
+
+    def cp(o, a):
+        op("v", lambda: g.vector.tensor_copy(o[0], a[0]), [o], [a], vcost(o, a))
+
+    def fill(o, c):
+        op("v", lambda: g.vector.memset(o[0], c), [o], [])
+
+    def red(o, a):
+        op("v", lambda: g.vector.tensor_reduce(o[0], a[0], AxisListType.X, Op.add), [o], [a])
+
+    def mm(o, l, r, start, stop):
+        me = op("t", lambda: g.tensor.matmul(o[0], l[0], r[0], start, stop), [o], [l, r], max(64, r[4]) * TCYC)
+        if start and o[1] in closed:
+            ops[me][3].setdefault(closed[o[1]], False)
+        if stop:
+            closed[o[1]] = me
+
+    def act(o, a, func, **kw):
+        op("s", lambda: g.scalar.activation(o[0], a[0], func, **kw), [o], [a], max(64, o[4]) * CYC)
+
+    def asel(o, a, pat, cop, base, cm):
+        op("g", lambda: g.affine_select(o[0], a[0], pat, cop, 0.0, base, cm), [o], [a], 0.17 + 2 * o[4] * CYC)
+
+    def iota(o, pat, base, cm, small=True):
+        if small:
+            op("g", lambda: g.iota(o[0], pat, base, cm, allow_small_or_imprecise_dtypes=True), [o], [])
+        else:
+            op("g", lambda: g.iota(o[0], pat, base, cm), [o], [])
+
+    def mat(name, k):
+        return v(name, 128 * k, 128 * k + 128)
+
+    lists, closed = {}, {}
+    X = (T.X[:, 0:2048], "X", 0, 2048)
+
+    op("y", lambda: g.sync.dma_start(T.Z0[:], T.vein[:]), [v("Z0")], [], 2.0, "d0", 16)
+    op("y", lambda: g.sync.dma_start(T.win[:], T.w[:]), [v("win")], [], 2.0, "d1", 16)
+    op("y", lambda: g.sync.dma_start(T.fin[:], T.front[:]), [v("fin")], [], 2.0, "d2", 16)
+    op("y", lambda: g.sync.dma_start(T.X[:, 0:2048], T.rock[:]), [X], [], 2.0, "d3", 16)
+    op("y", lambda: g.sync.dma_start(T.lin[:], T.lim[:]), [v("lin")], [], 2.0, "d4", 16)
+
+    fill(v("one"), 1.0)
+    iota(v("pi"), [[0, 1]], 0, 1, False)
+    asel(v("BD1"), v("one", 0, 128), [[-16, 8], [0, 16]], Op.is_ge, 0, 1)
+    asel(v("BD"), v("BD1"), [[16, 8], [0, 16]], Op.is_ge, 15, -1)
+    asel(v("I"), v("one", 0, 128), [[-1, 128]], Op.is_equal, 0, 1)
+    iota(v("RC", r=2), [[0, 8], [37, 16]], 0, 0)
+    for m in range(5):
+        fill(v("RM", 96 * m, 96 * m + 96, r=2), float(32 << m))
+        fill(v("RM", 96 * m, 96 * m + 96, r=1), float(m * (32 << m)))
+    fill(v("RC", r=1), 613.0)
+    ts(v("pk"), v("pi"), 15, Op.bitwise_and)
+    cp(v("kc"), v("pk"))
+    cp(v("F0"), v("fin"))
+    ts(v("w2c"), v("win"), 2.0, Op.mult)
+    ts(v("W2"), v("BD"), v("w2c"), Op.mult)
+    for m in range(5):
+        act(mat("I5", m), v("I"), Act.Copy, scale=float(32 << m))
+
+    def prep(t, ch):
+        kind, a, b = ch
+        n = b - a
+        F, Z = v("F%d" % t, a, b), v("Z%d" % t, a, b)
+        mm(v("pU", 0, n), v("W2"), Z, True, False)
+        mm(v("pU", 0, n), v("one", 0, 128, r=1), v("one", 0, n, r=1), False, True)
+        mm(v("pU", n, 2 * n), v("BD"), Z, True, True)
+        mm(v("pU", 2 * n, 3 * n), v("I"), F, True, True)
+        for m in range(5):
+            o = v("pR", m * n, m * n + n)
+            mm(o, v("RC", r=2), v("RM", 96 * m, 96 * m + n, r=2), True, False)
+            mm(o, mat("I5", m), F, False, True)
+        cp(v("usi", 2 * a, 2 * b), v("pU", 0, 2 * n))
+        ts(v("u2", a, b), v("usi", 2 * a, 2 * a + n), 4095, Op.bitwise_and)
+        tt(v("P", a, b), v("pU", 2 * n, 3 * n), v("u2", a, b), Op.mult)
+        for m in range(5):
+            cm = (5 * a + m * n, 5 * a + m * n + n)
+            tt(v("Q", *cm), v("pR", m * n, m * n + n), v("P", a, b), Op.add)
+            ts(v("C", *cm), v("Q", *cm), 5 + m, Op.logical_shift_right, 2047, Op.bitwise_and)
+            if kind == "S":
+                cp(v("off6", 6 * a + m, 6 * b - 5 + m, 6), v("C", *cm))
+        if kind == "V":
+            cp(v("offV", 0, 5 * n), v("C", 5 * a, 5 * b))
+        cp(v("c16", 5 * a, 5 * b), v("C", 5 * a, 5 * b))
+        ts(v("si", a, b), v("usi", 2 * a + n, 2 * b), 15, Op.bitwise_and)
+        ts(v("oh", a, b), v("si", a, b), v("kc"), Op.is_equal)
+        ts(v4("UH", t, a, b), v("u2", a, b), 0.5, Op.mult, -0.5, Op.add)
+        ts(v("zq", a, b), Z, 0.25, Op.mult, 1279.625, Op.add)
+        ts(v("Kn", a, b), F, float(KN), Op.add)
+
+    def spread(t, ch):
+        kind, a, b = ch
+        for k in range(16):
+            asel(v("Zx", k, 16 * (b - a) - 15 + k, 16), v("Z%d" % t, a, b), [[0, b - a]], Op.is_gt, 1, 0)
+
+    def gather_s(t, ch):
+        for i in range(ch[1], ch[2]):
+            def one(o, f, z):
+                op("s", lambda: g.scalar.activation(o[0], X[0].indirect(f[0]), Act.Abs, bias=z[0], scale=-1.0), [o], [X, f, z], 0.065 + 80 * GATH * CYC)
+            one(v("A", 80 * i, 80 * i + 80), v("off6", 6 * i, 6 * i + 5), v("Z%d" % t, i, i + 1))
+
+    def gather_v(t, ch):
+        n = ch[2] - ch[1]
+        for m in range(5):
+            def one(o, f, z):
+                op("v", lambda: g.vector.tensor_tensor(o[0], X[0].indirect(f[0]), z[0], Op.subtract), [o], [X, f, z], 0.05 + o[4] * GATH * CYC)
+            one(v("D", 16 * n * m, 16 * n * (m + 1)), v("offV", m * n, m * n + n), v("Zx", 0, 16 * n))
+
+    def abs_v(ch):
+        n, a = ch[2] - ch[1], 80 * ch[1]
+        for m in range(5):
+            act(v("A", a + 16 * n * m, a + 16 * n * (m + 1)), v("D", 16 * n * m, 16 * n * (m + 1)), Act.Abs)
+
+    def view5(name, kind, n, m, off=0):
+        if kind == "S":
+            return v(name, off + m, off + 5 * n - 4 + m, 5)
+        return v(name, off + m * n, off + m * n + n)
+
+    def score(ch):
+        kind, a, b = ch
+        n = b - a
+        step = SUB if kind == "S" else n
+        for p in range(a, b, step):
+            w, off = step, 5 * (p - a)
+            o, on = v("pS", off, off + 5 * w), v("pN", off, off + 5 * w)
+            mm(o, v("KC", r=2), v("MCS" if kind == "S" else "MCV", 0, 5 * w, r=2), True, False)
+            for m in range(5):
+                mm(view5("pS", kind, w, m, off), v("I"), v("c16", 5 * a + m * n + p - a, 5 * a + m * n + p - a + w), False, False)
+            for k in range(16):
+                mm(o, mat("ES", k), v("A", 80 * p + k, 80 * (p + w) - 15 + k, 16), False, k == 15)
+            pieces = 1 if kind == "S" else 5
+            for c in range(pieces):
+                x = (80 * p + c * 80 * w // pieces, 80 * p + (c + 1) * 80 * w // pieces)
+                ts(v("NR", *x), v("A", *x), v("top"), Op.is_le)
+            for k in range(16):
+                mm(on, mat("E", k), v("NR", 80 * p + k, 80 * (p + w) - 15 + k, 16), k == 0, k == 15)
+
+    def choose(t, ch):
+        kind, a, b = ch
+        n = b - a
+        KB = v("KB", a, b)
+        for m in range(5):
+            tt(KB, view5("pS", kind, n, m), KB if m else v("Kn", a, b), Op.min)
+        for m in range(5):
+            tt(view5("EQm", kind, n, m, 5 * a), view5("pS", kind, n, m), KB, Op.is_equal)
+        tt(v("TT", 5 * a, 5 * b), v("EQm", 5 * a, 5 * b), v("pN", 0, 5 * n), Op.mult)
+        cnt = v("pN", 416, 416 + n)
+        for m in range(5):
+            mm(cnt, v("I"), view5("TT", kind, n, m, 5 * a), m == 0, m == 4)
+        ts(v("nf", a, b), cnt, 8.5, Op.is_lt, float(1 << 25), Op.mult)
+        tt(v("K2", a, b), KB, v("nf", a, b), Op.add)
+        tt(v("KI", a, b), v("K2", a, b), v("Kn", a, b), Op.min)
+        ts(v4("FI", t, a, b), v("KI", a, b), 2047, Op.bitwise_and)
+
+    def meeting(t, gi):
+        a, b = GR[gi]
+        h = (b - a) // 2
+        q0, q1 = a // 2, b // 2
+        per = max(x for x in (1, 2, 4, 8, 16) if x * h <= 512)
+        rounds = [(r, "pA" if (r // per) % 2 == 0 else "pB") for r in range(0, 16, per)]
+        S, J = v("SJ", a, a + h), v("SJ", a + h, b)
+
+        def pr(name):
+            return v(name, q0, q1)
+
+        def big(name, k, c=1):
+            return v(name, 8 * a + k * h, 8 * a + (k + c) * h)
+        G, LM, XP, SN = (v("p1", 112 * i, 112 * i + h) for i in range(4))
+        ML, MT, JN = (v("p2", 112 * i, 112 * i + h) for i in range(3))
+        cp(S, v4("FI", t, a, b, 0))
+        cp(J, v4("FI", t, a, b, 1))
+        ts(v("Hh", a, b), v("SJ", a, b), 0.125, Op.mult, 1279.5625, Op.add)
+        for r, bank in rounds:
+            for l in range(per):
+                o = v(bank, l * h, l * h + h)
+                mm(o, mat("B", r + l), v("Hh", a, a + h), True, False)
+                mm(o, v("Ineg"), v("Hh", a + h, b), False, True)
+            ts(big("EQ2", r, per), v(bank, 0, per * h), 0.0, Op.is_equal)
+        for l in range(16):
+            mm(G, v("W32"), big("EQ2", l), l == 0, l == 15)
+        for l in range(16):
+            mm(ML, mat("Q4", l), big("EQ2", l), l == 0, l == 15)
+        tt(pr("JS"), J, S, Op.mult)
+        jq = v("pU", 320, 320 + h)
+        mm(jq, v("I32"), J, True, False)
+        mm(jq, v("I32"), v4("UH", t, a, b, 1), False, True)
+        tt(pr("JQ"), jq, pr("JS"), Op.add)
+        ts(pr("Jn"), pr("JQ"), 5, Op.logical_shift_right, 2047, Op.bitwise_and)
+        tt(pr("t1"), pr("Jn"), J, Op.subtract)
+        ts(pr("w1"), G, v("p33"), Op.is_ge)
+        ts(pr("mj"), G, v("p32"), Op.is_ge)
+        tt(pr("w0"), pr("mj"), pr("w1"), Op.subtract)
+        tt(pr("wM"), ML, pr("w0"), Op.mult)
+        mm(LM, v("BD"), pr("wM"), True, True)
+        ts(pr("ms"), LM, v("p4"), Op.is_ge)
+        mm(XP, v("BM"), pr("ms"), True, False)
+        mm(XP, v("BN"), pr("mj"), False, True)
+        ts(pr("x16"), XP, v("kx"), Op.add)
+        for r, bank in rounds:
+            for k in range(per):
+                mm(v(bank, k * h, k * h + h), mat("B", r + k), J, True, True)
+            for k in range(per):
+                ts(big("MK", r + k), pr("x16"), float(r + k), Op.is_equal)
+            tt(big("PJ", r, per), v(bank, 0, per * h), big("MK", r, per), Op.mult)
+        ts(pr("nv"), pr("x16"), 15.5, Op.is_gt)
+        tt(pr("nvS"), pr("nv"), S, Op.mult)
+        mm(SN, v("I"), pr("nvS"), True, False)
+        for k in range(16):
+            mm(SN, v("I"), big("PJ", k), False, k == 15)
+        tt(pr("t2"), pr("t1"), pr("mj"), Op.mult)
+        mm(JN, v("I"), J, True, False)
+        mm(JN, v("I"), pr("t2"), False, True)
+        mm(MT, v("S15"), pr("mj"), True, True)
+        cp(v4("FO", t, a, b, 1), JN)
+        cp(v4("FO", t, a, b, 0), SN)
+        red(v("metc", gi, gi + 1), MT)
+
+    def send(t, gi, what, src):
+        dst = T.cores[(rank + NEXT) % nrank]
+        rid, pid = topo.addr(dst, core)
+        es = topo.engines(core, dst)[:8]
+        a, b = GR[gi]
+        sem = "r%s%d%d" % (what, t + 1, gi)
+
+        def call():
+            g.remote_dma(out_ap=T["%s%d" % (what, t + 1)][:, a:b], in_ap=src[0], remote_sem=T.sem[sem], local_sem=T.sem["loc"],
+                         pid=pid, routing_id=rid, dma_engine_mask=sum(1 << e for e in es))
+        me = op("g", call, [], [src], 0.4, "loc", len(es))
+        ops.append(["r", None, WIRE, {me: False}, sem, len(topo.engines(T.cores[(rank - NEXT) % nrank], core)[:8])])
+        mark("%s%d" % (what, t + 1), a, b, True, len(ops) - 1)
+
+    def mining(t, gi):
+        a, b = GR[gi]
+        n, c0, c1 = b - a, a // 16, b // 16
+        FO, Z, o, f = v4("FO", t, a, b), v("Z%d" % t, a, b), v("Y", a, b), v("Ol", c0, c1)
+        OL, ER, VN, CN, LL = v("p2", 448, 448 + n // 16), v("pA", 0, n), v("pB", 0, n), v("pA", 256, 256 + n), v("p2", 480, 480 + n // 16)
+        if t < 3:
+            send(t, gi, "F", FO)
+        else:
+            cp(v("yo", a, b), FO)
+            op("y", lambda: g.sync.dma_start(T.yf[:, a:b], T.yo[:, a:b]), [], [v("yo", a, b)], 2.0, "oF%d" % gi, 16)
+        tt(v("Fm", a, b), FO, v("oh", a, b), Op.mult)
+        for q in range(16):
+            mm(OL, mat("E", q), v("Fm", a + q, b - 15 + q, 16), q == 0, q == 15)
+        mm(ER, v("BD"), v("Fm", a, b), True, True)
+        cp(f, OL)
+        cp(v("Ouf", c0, c1), OL)
+        cp(v("Er", a, b), ER)
+        op("s", lambda: g.scalar.activation(o[0], X[0].indirect(f[0]), Act.Copy), [o], [X, f], 0.065 + n * GATH * CYC)
+        if gi == len(GR) - 1:
+            for x in range(gi):
+                scatter(x)
+        mm(VN, v("Ihalf"), Z, True, False)
+        mm(VN, v("q9"), v("one", 0, n), False, False)
+        mm(VN, v("Ihalf"), o, False, True)
+        ts(v("zt", a, b), VN, 1280.0, Op.add)
+        ts(v("Zo%d" % t, a, b), v("zt", a, b), -1280.0, Op.add)
+        if t < 3:
+            send(t, gi, "Z", v("Zo%d" % t, a, b))
+        else:
+            op("y", lambda: g.sync.dma_start(T.yz[:, a:b], T["Zo3"][:, a:b]), [], [v("Zo3", a, b)], 2.0, "oZ%d" % gi, 16)
+
+        def later(c):
+            lo = max(16 * c, a)
+            w = (T.EQW[:, c, lo - 16 * c:b - 16 * c], "EQW", 256 * c + lo - 16 * c, 256 * c + b - 16 * c, b - lo)
+            return lo, w
+        for c in range(c1):
+            lo, w = later(c)
+            ts(w, v("Er", lo, b), v("Ouf", c, c + 1), Op.is_equal)
+        dg = (T.EQW[:, c0:c1, 0:16], "EQW", 256 * c0, 256 * c1, n)
+        op("v", lambda: g.vector.tensor_tensor(dg[0], dg[0], T.DM[:, c0:c1, :], Op.mult), [dg], [dg, ("", "DM", 0, 256)], 2 * n * CYC)
+        for c in range(c1):
+            lo, w = later(c)
+            mm(v("pA", 256 + lo - a, 256 + n), v("BD"), w, c == 0, c == c1 - 1)
+        act(v("lo", a, b), CN, Act.Sign)
+        for q in range(16):
+            mm(LL, mat("E", q), v("lo", a + q, b - 15 + q, 16), q == 0, q == 15)
+        tt(v("R1", a, b), o, v("zq", a, b), Op.subtract)
+        ts(v("R2", a, b), v("R1", a, b), 1280.0, Op.add, 0.0, Op.max)
+        tt(v("LI", c0, c1), LL, v("IO", c0, c1), Op.mult)
+        tt(v("LO", c0, c1), v("LI", c0, c1), v("Ouf", c0, c1), Op.max)
+        cp(v("Ls", c0, c1), v("LO", c0, c1))
+        lists[gi] = (v("Ls", c0, c1), v("R2", a, b))
+
+    def scatter(gi):
+        XW, ls, r2 = (T.X[:, 0:2304], "X", 0, 2304), lists[gi][0], lists[gi][1]
+        op("v", lambda: g.vector.tensor_copy(XW[0].indirect(ls[0]), r2[0]), [XW], [ls, r2], 0.05 + r2[4] * 3.8 * CYC)
+
+    def limits(t):
+        if t == 0:
+            cp(v("limf"), v("lin"))
+            cp(v("top"), v("limf"))
+        else:
+            red(v("mets"), v("metc", 0, len(GR)))
+            cp(v("meti"), v("mets"))
+            ts(v("mete"), v("meti"), 3, Op.bitwise_and)
+            tt(v("top"), v("limf"), v("mete"), Op.add)
+
+    def key_constants():
+        for k in range(16):
+            asel(mat("E", k), v("BD"), [[0, 8], [1, 16]], Op.is_equal, -k, 0)
+            act(mat("ES", k), mat("E", k), Act.Copy, scale=10240.0)
+        iota(v("KC", r=2), [[0, 128]], -4096, 6144)
+        iota(v("MCS", r=2), [[0, 96], [1, 5]], 0, 0)
+        iota(v("MCV", 0, 5 * NV, r=2), [[1, 5], [0, NV]], 0, 0)
+        fill(v("MCS", r=1), 4096.0)
+        fill(v("MCV", 0, 5 * NV, r=1), 4096.0)
+
+    def last_constants():
+        iota(v("io"), [[1, 16]], 0, 0)
+        op("g", lambda: g.iota(T.DMi[:], [[0, 16], [1, 16]], 0, 0, allow_small_or_imprecise_dtypes=True), [("", "DMi", 0, 256)], [])
+        iota(v("IO"), [[1, 16]], 128, 0)
+        ts(v("Ineg"), v("I"), -1.0, Op.mult)
+        ts(v("I32"), v("I"), 32.0, Op.mult)
+        ts(v("Ihalf"), v("I"), 0.5, Op.mult)
+        fill(v("q9"), -(2.0 ** -9))
+        ts(v("OH"), v("io"), v("kc"), Op.is_equal)
+        for l in range(16):
+            ts(mat("B", l), v("BD"), v("OH", l, l + 1), Op.mult)
+            act(mat("Q4", l), v("I"), Act.Copy, scale=float(4 ** (15 - l)))
+        for r in range(16):
+            fill(v("PW", r, r + 1), 2.0 ** (5 * (15 - r)))
+            fill(v("PW", 16 + r, 17 + r), 2.0 ** (2 * (16 - r)))
+        for j, name in ((0, "p32"), (16, "p4")):
+            tt(v("PT", j, j + 16), v("PW", j, j + 16), v("OH"), Op.mult)
+            red(v(name), v("PT", j, j + 16))
+        ts(v("p33"), v("p32"), 32.0, Op.mult)
+        ts(v("W32"), v("BD"), v("p32"), Op.mult)
+        ts(v("BN"), v("BD"), -1.0, Op.mult)
+        ts(v("BD1"), v("I"), -64.0, Op.mult)
+        tt(v("BM"), v("BD1"), v("BD"), Op.add)
+        ts(v("S15"), v("one", 0, 128), v("OH", 15, 16), Op.mult)
+        ts(v("kx"), v("kc"), 65.0, Op.add)
+        op("v", lambda: g.vector.tensor_scalar(T.DM[:], T.DMi[:], v("kc")[0], None, Op.is_gt), [("", "DM", 0, 256)], [("", "DMi", 0, 256), v("kc")], 256 * CYC)
+        ts(v("PT", 32, 33), v("kc"), 0.0625, Op.mult)
+        ts(v("IO"), v("IO"), v("PT", 32, 33), Op.add)
+
+    vch = [ch for ch in CH if ch[0] == "V"][0]
+    for t in range(4):
+        if t == 0:
+            for ch in CH:
+                prep(0, ch)
+            key_constants()
+            last_constants()
+        else:
+            for ch in CH:
+                if ch[1] >= GR[-1][0]:
+                    prep(t, ch)
+        spread(t, vch)
+        for ch in CH:
+            if ch[0] == "S":
+                gather_s(t, ch)
+        gather_v(t, vch)
+        limits(t)
+        abs_v(vch)
+        for gi, (a, b) in enumerate(GR):
+            for ch in CH:
+                if a <= ch[1] < b:
+                    score(ch)
+                    choose(t, ch)
+            meeting(t, gi)
+            mining(t, gi)
+            if gi == len(GR) - 1:
+                scatter(gi)
+            elif t < 3:
+                for ch in CH:
+                    if a <= ch[1] < b:
+                        prep(t + 1, ch)
+    op("y", lambda: g.sync.dma_start(T.yx[:], T.X[:, 0:2048]), [], [X], 2.0, "d3", 16)
+
+    succ = [[] for _ in ops]
+    left = [0] * len(ops)
+    for i, o in enumerate(ops):
+        for j in o[3]:
+            succ[j].append(i)
+            left[i] += 1
+    way = [0.0] * len(ops)
+    for i in range(len(ops) - 1, -1, -1):
+        best = 0.0
+        for j in succ[i]:
+            best = max(best, way[j] + (WAKE if ops[j][3][i] else 0.0))
+        way[i] = best + ops[i][2]
+    free, ready = {}, {}
+    early = [0.0] * len(ops)
+    for i, o in enumerate(ops):
+        free[o[0]] = 0.0
+        ready.setdefault(o[0], [])
+        if not left[i]:
+            ready[o[0]].append(i)
+    order = []
+    while len(order) < len(ops):
+        pick = None
+        for q, r in ready.items():
+            if r:
+                start = max(free[q], min(early[i] for i in r))
+                if pick is None or start < pick[0]:
+                    pick = (start, q)
+        start, q = pick
+        i = max((i for i in ready[q] if early[i] <= start + 1e-9), key=lambda i: way[i])
+        ready[q].remove(i)
+        end = start + ops[i][2]
+        if q != "r":
+            free[q] = end if q != "y" else start + 0.1
+        order.append(i)
+        for j in succ[i]:
+            left[j] -= 1
+            early[j] = max(early[j], end + WAKE if ops[j][3][i] else (end if ops[j][0] == "r" else start))
+            if not left[j]:
+                ready[ops[j][0]].append(j)
+
+    count, know, value, clocks = {}, {q: {} for q in free}, {}, {}
+    for i in order:
+        q, fn, cost, deps, sem, inc = ops[i]
+        k = know[q]
+        best = {}
+        for j, wait in deps.items():
+            if wait and (ops[j][4] not in best or value[best[ops[j][4]]] < value[j]):
+                best[ops[j][4]] = j
+        for j in sorted(best.values(), key=lambda j: -len(clocks[j])):
+            if k.get(ops[j][4], 0) < value[j]:
+                eng[q].wait_ge(T.sem[ops[j][4]], value[j])
+                for s, x in clocks[j].items():
+                    if k.get(s, 0) < x:
+                        k[s] = x
+        count[sem] = value[i] = count.get(sem, 0) + inc
+        clocks[i] = {sem: value[i]}
+        if q != "r":
+            r = fn()
+            if r is not None:
+                r.then_inc(T.sem[sem], inc)
+            clocks[i] = dict(k)
+            clocks[i][sem] = value[i]
+    for s in SEMAPHORES:
+        if count.get(s):
+            g.wait_ge(T.sem[s], count[s])

@@ -9,33 +9,31 @@ KN = 2956 * 10240 - (1 << 24)
 
 f32, bf, f16, i32, u16 = "float32", "bfloat16", "float16", "int32", "uint16"
 SCRATCH = {
-    "X": ("sbuf", [128, 2304], bf), "fin": ("sbuf", [128, 256], i32), "win": ("sbuf", [128, 1], i32), "lin": ("sbuf", [128, 1], i32),
+    "X": ("sbuf", [128, 2560], bf), "fin": ("sbuf", [128, 256], i32), "win": ("sbuf", [128, 1], i32), "lin": ("sbuf", [128, 1], i32),
     "A": ("sbuf", [128, 20480], bf), "D": ("sbuf", [128, 80 * NV], bf), "NR": ("sbuf", [128, 20480], bf), "Zx": ("sbuf", [128, 16 * NV], bf),
     "off6": ("sbuf", [128, 1536], u16), "offV": ("sbuf", [128, 5 * NV], u16), "c16": ("sbuf", [128, 1280], f16),
-    "usi": ("sbuf", [128, 512], i32), "u2": ("sbuf", [128, 256], i32), "si": ("sbuf", [128, 256], i32), "oh": ("sbuf", [128, 256], f16),
+    "usi": ("sbuf", [128, 512], i32), "u2": ("sbuf", [128, 256], i32), "si": ("sbuf", [128, 256], i32),
     "zq": ("sbuf", [128, 256], f16), "P": ("sbuf", [128, 256], f32), "Q": ("sbuf", [128, 1280], i32), "C": ("sbuf", [128, 1280], i32),
     "Kn": ("sbuf", [128, 256], f32), "KB": ("sbuf", [128, 256], f32), "EQm": ("sbuf", [128, 1280], bf), "TT": ("sbuf", [128, 1280], bf),
-    "nf": ("sbuf", [128, 256], f32), "K2": ("sbuf", [128, 256], f32), "KI": ("sbuf", [128, 256], i32),
+    "KF": ("sbuf", [128, 256], f32), "K1": ("sbuf", [128, 256], f32), "K2": ("sbuf", [128, 256], f32), "KI": ("sbuf", [128, 256], i32),
     "SJ": ("sbuf", [128, 256], f16), "Hh": ("sbuf", [128, 256], f16), "EQ2": ("sbuf", [128, 2048], bf), "MK": ("sbuf", [128, 2048], f16),
-    "PJ": ("sbuf", [128, 2048], f16), "mj": ("sbuf", [128, 128], bf), "w1": ("sbuf", [128, 128], bf), "w0": ("sbuf", [128, 128], bf),
-    "wM": ("sbuf", [128, 128], bf), "ms": ("sbuf", [128, 128], bf), "x16": ("sbuf", [128, 128], f16), "nv": ("sbuf", [128, 128], f16),
-    "nvS": ("sbuf", [128, 128], f16), "JS": ("sbuf", [128, 128], f32), "JQ": ("sbuf", [128, 128], i32), "Jn": ("sbuf", [128, 128], i32),
-    "t1": ("sbuf", [128, 128], f16), "t2": ("sbuf", [128, 128], f16), "metc": ("sbuf", [128, 4], f32),
-    "Fm": ("sbuf", [128, 256], f16), "Er": ("sbuf", [128, 256], f16), "Ouf": ("sbuf", [128, 16], f32), "Ol": ("sbuf", [128, 16], u16),
+    "PJ": ("sbuf", [128, 2048], f16), "LT": ("sbuf", [128, 128], bf), "KX": ("sbuf", [128, 16], f32), "ph": ("sbuf", [128, 768], f16),
+    "pb": ("sbuf", [128, 512], bf), "JS": ("sbuf", [128, 128], f32), "JQ": ("sbuf", [128, 128], i32), "Jn": ("sbuf", [128, 128], i32),
+    "metc": ("sbuf", [128, 4], f32), "Er": ("sbuf", [128, 256], f16), "Ouf": ("sbuf", [128, 16], f32), "Ol": ("sbuf", [128, 16], u16),
     "Y": ("sbuf", [128, 256], bf), "zt": ("sbuf", [128, 256], f16), "R1": ("sbuf", [128, 256], f16), "R2": ("sbuf", [128, 256], bf),
-    "EQW": ("sbuf", [128, 16, 256], bf), "lo": ("sbuf", [128, 256], bf), "LI": ("sbuf", [128, 16], f32), "LO": ("sbuf", [128, 16], f32),
+    "EQW": ("sbuf", [128, 16, 256], bf), "lo": ("sbuf", [128, 256], bf), "LO": ("sbuf", [128, 16], f32),
     "Ls": ("sbuf", [128, 16], u16), "yo": ("sbuf", [128, 256], f32),
     "one": ("sbuf", [128, 512], bf), "BD": ("sbuf", [128, 128], bf), "BD1": ("sbuf", [128, 128], bf), "I": ("sbuf", [128, 128], bf),
-    "Ineg": ("sbuf", [128, 128], bf), "I32": ("sbuf", [128, 128], bf), "Ihalf": ("sbuf", [128, 128], bf), "q9": ("sbuf", [128, 128], bf),
+    "I25": ("sbuf", [128, 128], bf), "c85": ("sbuf", [128, 128], bf), "c16k": ("sbuf", [128, 128], bf), "I32": ("sbuf", [128, 128], bf), "Ihalf": ("sbuf", [128, 128], bf), "q9": ("sbuf", [128, 128], bf),
     "I5": ("sbuf", [128, 640], bf), "E": ("sbuf", [128, 2048], bf), "ES": ("sbuf", [128, 2048], bf), "B": ("sbuf", [128, 2048], bf),
     "Q4": ("sbuf", [128, 2048], bf), "W2": ("sbuf", [128, 128], bf), "W32": ("sbuf", [128, 128], bf), "BM": ("sbuf", [128, 128], bf),
     "BN": ("sbuf", [128, 128], bf), "S15": ("sbuf", [128, 128], bf), "KC": ("sbuf", [128, 128], bf), "MCS": ("sbuf", [128, 480], bf),
     "MCV": ("sbuf", [128, 480], bf), "RC": ("sbuf", [128, 128], f16), "RM": ("sbuf", [128, 480], f16), "io": ("sbuf", [128, 16], f32),
     "OH": ("sbuf", [128, 16], f32), "PW": ("sbuf", [128, 48], f32), "PT": ("sbuf", [128, 48], f32), "DMi": ("sbuf", [128, 16, 16], f32),
-    "DM": ("sbuf", [128, 16, 16], bf), "IO": ("sbuf", [128, 16], f32),
+    "DM": ("sbuf", [128, 16, 16], bf), "IO": ("sbuf", [128, 16], f16),
 }
 COLS = {}
-for _b, _d, _ns in (("colf", f32, ("kc", "kx", "w2c", "p32", "p33", "p4", "limf", "top", "mets")), ("coli", i32, ("pi", "pk", "meti", "mete"))):
+for _b, _d, _ns in (("colf", f32, ("kc", "kx", "w2c", "p32", "p4", "limf", "top", "mets")), ("coli", i32, ("pi", "pk", "meti", "mete"))):
     SCRATCH[_b] = ("sbuf", [128, len(_ns)], _d)
     for _i, _n in enumerate(_ns):
         COLS[_n] = (_b, _i)
@@ -43,7 +41,7 @@ for _t in range(4):
     SCRATCH["F%d" % _t] = ("sbuf", [128, 256], f16)
     SCRATCH["Z%d" % _t] = ("sbuf", [128, 256], bf)
     SCRATCH["Zo%d" % _t] = ("sbuf", [128, 256], bf)
-    for _n, _d in (("UH", f16), ("FI", i32), ("FO", f16)):
+    for _n, _d in (("UH", f16), ("OP", f16), ("FI", i32), ("FO", f16), ("Fm", f16)):
         SCRATCH["%s%d" % (_n, _t)] = ("sbuf", [128, 128 >> _t, 2, 1 << _t], _d)
 BANKS = ["pU", "pR", "pS", "pN", "pA", "pB", "p1", "p2"]
 for _n in BANKS:
@@ -51,7 +49,7 @@ for _n in BANKS:
 SEMAPHORES = ["sg", "sv", "ss", "st", "loc"] + ["d%d" % i for i in range(5)] + ["o%s%d" % (c, h) for c in "FZ" for h in range(len(GR))] + \
     ["r%s%d%d" % (c, t, h) for c in "FZ" for t in (1, 2, 3) for h in range(len(GR))]
 
-CYC, TCYC, GATH, WAKE, WIRE = 1.04e-3, 0.52e-3, 1.56, 0.07, 3.0
+CYC, TCYC, GATH, WAKE, WIRE = 1.04e-3, 0.52e-3, 1.56, 0.22, 3.0
 
 
 def rank_program(g, core, T, topo):
@@ -85,8 +83,8 @@ def rank_program(g, core, T, topo):
         h = hist.setdefault(name, [])
         if wr and name not in BANKS:
             h[:] = [a for a in h if not (lo <= a[1] and a[2] <= hi)]
-        elif name in BANKS:
-            h[:] = [a for a in h if not (lo <= a[1] and a[2] <= hi and ops[a[3]][0] == ops[me][0] and (wr or not a[0]))]
+        elif wr:
+            h[:] = [a for a in h if not (lo <= a[1] and a[2] <= hi and ops[a[3]][0] == ops[me][0])]
         h.append((wr, lo, hi, me))
 
     def v(name, lo=0, hi=None, st=1, r=128):
@@ -203,7 +201,7 @@ def rank_program(g, core, T, topo):
             cp(v("offV", 0, 5 * n), v("C", 5 * a, 5 * b))
         cp(v("c16", 5 * a, 5 * b), v("C", 5 * a, 5 * b))
         ts(v("si", a, b), v("usi", 2 * a + n, 2 * b), 15, Op.bitwise_and)
-        ts(v("oh", a, b), v("si", a, b), v("kc"), Op.is_equal)
+        ts(v4("OP", t, a, b), v("si", a, b), v("kc"), Op.is_equal)
         ts(v4("UH", t, a, b), v("u2", a, b), 0.5, Op.mult, -0.5, Op.add)
         ts(v("zq", a, b), Z, 0.25, Op.mult, 1279.625, Op.add)
         ts(v("Kn", a, b), F, float(KN), Op.add)
@@ -240,14 +238,14 @@ def rank_program(g, core, T, topo):
         kind, a, b = ch
         n = b - a
         step = SUB if kind == "S" else n
+        mm(v("pS", 0, 5 * n), v("KC", r=2), v("MCS" if kind == "S" else "MCV", 0, 5 * n, r=2), True, False)
+        for m in range(5):
+            mm(view5("pS", kind, n, m), v("I"), v("c16", 5 * a + m * n, 5 * a + m * n + n), False, False)
         for p in range(a, b, step):
             w, off = step, 5 * (p - a)
             o, on = v("pS", off, off + 5 * w), v("pN", off, off + 5 * w)
-            mm(o, v("KC", r=2), v("MCS" if kind == "S" else "MCV", 0, 5 * w, r=2), True, False)
-            for m in range(5):
-                mm(view5("pS", kind, w, m, off), v("I"), v("c16", 5 * a + m * n + p - a, 5 * a + m * n + p - a + w), False, False)
             for k in range(16):
-                mm(o, mat("ES", k), v("A", 80 * p + k, 80 * (p + w) - 15 + k, 16), False, k == 15)
+                mm(o, mat("ES", k), v("A", 80 * p + k, 80 * (p + w) - 15 + k, 16), False, k == 15 and p + w == b)
             pieces = 1 if kind == "S" else 5
             for c in range(pieces):
                 x = (80 * p + c * 80 * w // pieces, 80 * p + (c + 1) * 80 * w // pieces)
@@ -259,17 +257,22 @@ def rank_program(g, core, T, topo):
         kind, a, b = ch
         n = b - a
         KB = v("KB", a, b)
-        for m in range(5):
-            tt(KB, view5("pS", kind, n, m), KB if m else v("Kn", a, b), Op.min)
+        K1, K2 = v("K1", a, b), v("K2", a, b)
+        tt(K1, view5("pS", kind, n, 0), v("Kn", a, b), Op.min)
+        tt(K2, view5("pS", kind, n, 1), v("Kn", a, b), Op.min)
+        tt(K1, view5("pS", kind, n, 2), K1, Op.min)
+        tt(K2, view5("pS", kind, n, 3), K2, Op.min)
+        tt(K1, view5("pS", kind, n, 4), K1, Op.min)
+        tt(KB, K1, K2, Op.min)
         for m in range(5):
             tt(view5("EQm", kind, n, m, 5 * a), view5("pS", kind, n, m), KB, Op.is_equal)
         tt(v("TT", 5 * a, 5 * b), v("EQm", 5 * a, 5 * b), v("pN", 0, 5 * n), Op.mult)
         cnt = v("pN", 416, 416 + n)
         for m in range(5):
-            mm(cnt, v("I"), view5("TT", kind, n, m, 5 * a), m == 0, m == 4)
-        ts(v("nf", a, b), cnt, 8.5, Op.is_lt, float(1 << 25), Op.mult)
-        tt(v("K2", a, b), KB, v("nf", a, b), Op.add)
-        tt(v("KI", a, b), v("K2", a, b), v("Kn", a, b), Op.min)
+            mm(cnt, v("I25"), view5("TT", kind, n, m, 5 * a), m == 0, False)
+        mm(cnt, v("c85", r=1), v("one", 0, n, r=1), False, True)
+        tt(v("KF", a, b), cnt, KB, Op.max)
+        tt(v("KI", a, b), v("KF", a, b), v("Kn", a, b), Op.min)
         ts(v4("FI", t, a, b), v("KI", a, b), 2047, Op.bitwise_and)
 
     def meeting(t, gi):
@@ -281,25 +284,34 @@ def rank_program(g, core, T, topo):
         S, J = v("SJ", a, a + h), v("SJ", a + h, b)
 
         def pr(name):
+            for buf, names in (("ph", ("nv", "nvS", "t1", "t2", "ohS", "ohJ")), ("pb", ("mj", "w0", "wM", "ms"))):
+                if name in names:
+                    return v(buf, 128 * names.index(name) + q0, 128 * names.index(name) + q1)
             return v(name, q0, q1)
 
         def big(name, k, c=1):
             return v(name, 8 * a + k * h, 8 * a + (k + c) * h)
         G, LM, XP, SN = (v("p1", 112 * i, 112 * i + h) for i in range(4))
+        HF = v("pN", 416, 416 + h)
         ML, MT, JN = (v("p2", 112 * i, 112 * i + h) for i in range(3))
+        ts(v("Hh", a, a + h), v4("FI", t, a, b, 0), 0.125, Op.mult, 1279.5625, Op.add)
+        ts(v("Hh", a + h, b), v4("FI", t, a, b, 1), 0.125, Op.mult, 1279.5625, Op.add)
         cp(S, v4("FI", t, a, b, 0))
         cp(J, v4("FI", t, a, b, 1))
-        ts(v("Hh", a, b), v("SJ", a, b), 0.125, Op.mult, 1279.5625, Op.add)
         for r, bank in rounds:
             for l in range(per):
                 o = v(bank, l * h, l * h + h)
-                mm(o, mat("B", r + l), v("Hh", a, a + h), True, False)
-                mm(o, v("Ineg"), v("Hh", a + h, b), False, True)
-            ts(big("EQ2", r, per), v(bank, 0, per * h), 0.0, Op.is_equal)
+                mm(o, mat("B", r + l), v("Hh", a, a + h), True, True)
+            for l in range(per):
+                tt(big("EQ2", r + l), v(bank, l * h, l * h + h), v("Hh", a + h, b), Op.is_equal)
         for l in range(16):
-            mm(G, v("W32"), big("EQ2", l), l == 0, l == 15)
+            mm(HF, v("LT"), big("EQ2", l), l == 0, l == 15)
         for l in range(16):
             mm(ML, mat("Q4", l), big("EQ2", l), l == 0, l == 15)
+        for l in range(16):
+            mm(G, v("W32"), big("EQ2", l), l == 0, l == 15)
+        cp(pr("ohS"), v4("OP", t, a, b, 0))
+        cp(pr("ohJ"), v4("OP", t, a, b, 1))
         tt(pr("JS"), J, S, Op.mult)
         jq = v("pU", 320, 320 + h)
         mm(jq, v("I32"), J, True, False)
@@ -307,22 +319,20 @@ def rank_program(g, core, T, topo):
         tt(pr("JQ"), jq, pr("JS"), Op.add)
         ts(pr("Jn"), pr("JQ"), 5, Op.logical_shift_right, 2047, Op.bitwise_and)
         tt(pr("t1"), pr("Jn"), J, Op.subtract)
-        ts(pr("w1"), G, v("p33"), Op.is_ge)
-        ts(pr("mj"), G, v("p32"), Op.is_ge)
-        tt(pr("w0"), pr("mj"), pr("w1"), Op.subtract)
+        ts(pr("w0"), HF, 0.0, Op.is_gt)
         tt(pr("wM"), ML, pr("w0"), Op.mult)
+        ts(pr("mj"), G, v("p32"), Op.is_ge)
         mm(LM, v("BD"), pr("wM"), True, True)
         ts(pr("ms"), LM, v("p4"), Op.is_ge)
         mm(XP, v("BM"), pr("ms"), True, False)
         mm(XP, v("BN"), pr("mj"), False, True)
-        ts(pr("x16"), XP, v("kx"), Op.add)
         for r, bank in rounds:
             for k in range(per):
                 mm(v(bank, k * h, k * h + h), mat("B", r + k), J, True, True)
             for k in range(per):
-                ts(big("MK", r + k), pr("x16"), float(r + k), Op.is_equal)
+                ts(big("MK", r + k), XP, v("KX", r + k, r + k + 1), Op.is_equal)
             tt(big("PJ", r, per), v(bank, 0, per * h), big("MK", r, per), Op.mult)
-        ts(pr("nv"), pr("x16"), 15.5, Op.is_gt)
+        ts(pr("nv"), XP, v("KX", 15, 16), Op.is_gt)
         tt(pr("nvS"), pr("nv"), S, Op.mult)
         mm(SN, v("I"), pr("nvS"), True, False)
         for k in range(16):
@@ -331,6 +341,8 @@ def rank_program(g, core, T, topo):
         mm(JN, v("I"), J, True, False)
         mm(JN, v("I"), pr("t2"), False, True)
         mm(MT, v("S15"), pr("mj"), True, True)
+        tt(v4("Fm", t, a, b, 1), JN, pr("ohJ"), Op.mult)
+        tt(v4("Fm", t, a, b, 0), SN, pr("ohS"), Op.mult)
         cp(v4("FO", t, a, b, 1), JN)
         cp(v4("FO", t, a, b, 0), SN)
         red(v("metc", gi, gi + 1), MT)
@@ -359,10 +371,11 @@ def rank_program(g, core, T, topo):
         else:
             cp(v("yo", a, b), FO)
             op("y", lambda: g.sync.dma_start(T.yf[:, a:b], T.yo[:, a:b]), [], [v("yo", a, b)], 2.0, "oF%d" % gi, 16)
-        tt(v("Fm", a, b), FO, v("oh", a, b), Op.mult)
+        w = 2 << t
         for q in range(16):
-            mm(OL, mat("E", q), v("Fm", a + q, b - 15 + q, 16), q == 0, q == 15)
-        mm(ER, v("BD"), v("Fm", a, b), True, True)
+            col = (T["Fm%d" % t][:, a // w + q // w:b // w:16 // w, q % w // (w // 2), q % (w // 2)], "Fm%d" % t, a, b, n // 16)
+            mm(OL, mat("E", q), col, q == 0, q == 15)
+        mm(ER, v("BD"), v4("Fm", t, a, b), True, True)
         cp(f, OL)
         cp(v("Ouf", c0, c1), OL)
         cp(v("Er", a, b), ER)
@@ -393,17 +406,18 @@ def rank_program(g, core, T, topo):
             lo, w = later(c)
             mm(v("pA", 256 + lo - a, 256 + n), v("BD"), w, c == 0, c == c1 - 1)
         act(v("lo", a, b), CN, Act.Sign)
+        mm(LL, v("I"), v("IO", c0, c1), True, False)
+        mm(LL, v("c16k", r=1), v("one", 0, n // 16, r=1), False, False)
         for q in range(16):
-            mm(LL, mat("E", q), v("lo", a + q, b - 15 + q, 16), q == 0, q == 15)
+            mm(LL, mat("ES", q), v("lo", a + q, b - 15 + q, 16), False, q == 15)
         tt(v("R1", a, b), o, v("zq", a, b), Op.subtract)
         ts(v("R2", a, b), v("R1", a, b), 1280.0, Op.add, 0.0, Op.max)
-        tt(v("LI", c0, c1), LL, v("IO", c0, c1), Op.mult)
-        tt(v("LO", c0, c1), v("LI", c0, c1), v("Ouf", c0, c1), Op.max)
+        tt(v("LO", c0, c1), LL, v("Ouf", c0, c1), Op.max)
         cp(v("Ls", c0, c1), v("LO", c0, c1))
         lists[gi] = (v("Ls", c0, c1), v("R2", a, b))
 
     def scatter(gi):
-        XW, ls, r2 = (T.X[:, 0:2304], "X", 0, 2304), lists[gi][0], lists[gi][1]
+        XW, ls, r2 = (T.X[:, 0:2560], "X", 0, 2560), lists[gi][0], lists[gi][1]
         op("v", lambda: g.vector.tensor_copy(XW[0].indirect(ls[0]), r2[0]), [XW], [ls, r2], 0.05 + r2[4] * 3.8 * CYC)
 
     def limits(t):
@@ -429,8 +443,9 @@ def rank_program(g, core, T, topo):
     def last_constants():
         iota(v("io"), [[1, 16]], 0, 0)
         op("g", lambda: g.iota(T.DMi[:], [[0, 16], [1, 16]], 0, 0, allow_small_or_imprecise_dtypes=True), [("", "DMi", 0, 256)], [])
-        iota(v("IO"), [[1, 16]], 128, 0)
-        ts(v("Ineg"), v("I"), -1.0, Op.mult)
+        act(v("I25"), v("I"), Act.Copy, scale=-float(1 << 25))
+        fill(v("c85"), 8.5 * (1 << 25))
+        fill(v("c16k"), -163840.0)
         ts(v("I32"), v("I"), 32.0, Op.mult)
         ts(v("Ihalf"), v("I"), 0.5, Op.mult)
         fill(v("q9"), -(2.0 ** -9))
@@ -444,16 +459,20 @@ def rank_program(g, core, T, topo):
         for j, name in ((0, "p32"), (16, "p4")):
             tt(v("PT", j, j + 16), v("PW", j, j + 16), v("OH"), Op.mult)
             red(v(name), v("PT", j, j + 16))
-        ts(v("p33"), v("p32"), 32.0, Op.mult)
+        asel(v("LT"), v("BD"), [[1, 128]], Op.is_gt, 0, -1)
+        ts(v("LT"), v("LT"), -32.0, Op.mult)
+        tt(v("LT"), v("LT"), v("I"), Op.add)
         ts(v("W32"), v("BD"), v("p32"), Op.mult)
         ts(v("BN"), v("BD"), -1.0, Op.mult)
         ts(v("BD1"), v("I"), -64.0, Op.mult)
         tt(v("BM"), v("BD1"), v("BD"), Op.add)
         ts(v("S15"), v("one", 0, 128), v("OH", 15, 16), Op.mult)
         ts(v("kx"), v("kc"), 65.0, Op.add)
+        ts(v("KX"), v("io"), v("kx"), Op.subtract)
         op("v", lambda: g.vector.tensor_scalar(T.DM[:], T.DMi[:], v("kc")[0], None, Op.is_gt), [("", "DM", 0, 256)], [("", "DMi", 0, 256), v("kc")], 256 * CYC)
-        ts(v("PT", 32, 33), v("kc"), 0.0625, Op.mult)
-        ts(v("IO"), v("IO"), v("PT", 32, 33), Op.add)
+        ts(v("PT", 16, 32), v("io"), 32.0, Op.mult, 2048.0, Op.add)
+        ts(v("PT", 32, 33), v("kc"), 2.0, Op.mult)
+        ts(v("IO"), v("PT", 16, 32), v("PT", 32, 33), Op.add)
 
     vch = [ch for ch in CH if ch[0] == "V"][0]
     for t in range(4):

from concourse.mybir import dt, AluOpType as Op, AxisListType, ActivationFunctionType as Act

NEXT = 1
CH = [("S", 0, 64), ("V", 64, 128), ("S", 128, 192), ("S", 192, 256)]
GR = [(0, 128), (128, 256)]
NV = [b - a for k, a, b in CH if k == "V"][0]
SUB = 16
KN = 2956 * 10240 - (1 << 24)

f32, bf, f16, i32, u16 = "float32", "bfloat16", "float16", "int32", "uint16"
SCRATCH = {
    "X": ("sbuf", [128, 2560], bf), "fin": ("sbuf", [128, 256], i32), "win": ("sbuf", [128, 1], i32), "lin": ("sbuf", [128, 1], i32),
    "A": ("sbuf", [128, 20480], bf), "D": ("sbuf", [128, 80 * NV], bf), "NR": ("sbuf", [128, 20480], bf), "Zx": ("sbuf", [128, 16 * NV], bf),
    "off6": ("sbuf", [128, 1536], u16), "offV": ("sbuf", [128, 5 * NV], u16), "c16": ("sbuf", [128, 1280], f16),
    "usi": ("sbuf", [128, 512], i32), "u2": ("sbuf", [128, 256], i32), "si": ("sbuf", [128, 256], i32),
    "zq": ("sbuf", [128, 256], f16), "P": ("sbuf", [128, 256], f32), "Q": ("sbuf", [128, 1280], i32), "C": ("sbuf", [128, 1280], i32),
    "Kn": ("sbuf", [128, 256], f32), "KB": ("sbuf", [128, 256], f32), "EQm": ("sbuf", [128, 1280], bf), "TT": ("sbuf", [128, 1280], bf),
    "KF": ("sbuf", [128, 256], f32), "K1": ("sbuf", [128, 256], f32), "K2": ("sbuf", [128, 256], f32), "KI": ("sbuf", [128, 256], i32),
    "SJ": ("sbuf", [128, 256], f16), "Hh": ("sbuf", [128, 256], f16), "EQ2": ("sbuf", [128, 2048], bf), "MK": ("sbuf", [128, 2048], f16),
    "PJ": ("sbuf", [128, 2048], f16), "LT": ("sbuf", [128, 128], bf), "KX": ("sbuf", [128, 16], f32), "ph": ("sbuf", [128, 768], f16),
    "pb": ("sbuf", [128, 512], bf), "JS": ("sbuf", [128, 128], f32), "JQ": ("sbuf", [128, 128], i32), "Jn": ("sbuf", [128, 128], i32),
    "metc": ("sbuf", [128, 4], f32), "Er": ("sbuf", [128, 256], f16), "Ouf": ("sbuf", [128, 16], f32), "Ol": ("sbuf", [128, 16], u16),
    "Y": ("sbuf", [128, 256], bf), "zt": ("sbuf", [128, 256], f16), "R1": ("sbuf", [128, 256], f16), "R2": ("sbuf", [128, 256], bf),
    "EQW": ("sbuf", [128, 16, 256], bf), "lo": ("sbuf", [128, 256], bf), "LO": ("sbuf", [128, 16], f32),
    "Ls": ("sbuf", [128, 16], u16), "yo": ("sbuf", [128, 256], f32),
    "one": ("sbuf", [128, 512], bf), "BD": ("sbuf", [128, 128], bf), "BD1": ("sbuf", [128, 128], bf), "I": ("sbuf", [128, 128], bf),
    "I25": ("sbuf", [128, 128], bf), "c85": ("sbuf", [128, 128], bf), "c16k": ("sbuf", [128, 128], bf), "I32": ("sbuf", [128, 128], bf), "Ihalf": ("sbuf", [128, 128], bf), "q9": ("sbuf", [128, 128], bf),
    "I5": ("sbuf", [128, 640], bf), "E": ("sbuf", [128, 2048], bf), "ES": ("sbuf", [128, 2048], bf), "B": ("sbuf", [128, 2048], bf),
    "Q4": ("sbuf", [128, 2048], bf), "W2": ("sbuf", [128, 128], bf), "W32": ("sbuf", [128, 128], bf), "BM": ("sbuf", [128, 128], bf),
    "BN": ("sbuf", [128, 128], bf), "S15": ("sbuf", [128, 128], bf), "KC": ("sbuf", [128, 128], bf), "MCS": ("sbuf", [128, 480], bf),
    "MCV": ("sbuf", [128, 480], bf), "RC": ("sbuf", [128, 128], f16), "RM": ("sbuf", [128, 480], f16), "io": ("sbuf", [128, 16], f32),
    "OH": ("sbuf", [128, 16], f32), "PW": ("sbuf", [128, 48], f32), "PT": ("sbuf", [128, 48], f32), "DMi": ("sbuf", [128, 16, 16], f32),
    "DM": ("sbuf", [128, 16, 16], bf), "IO": ("sbuf", [128, 16], f16),
}
COLS = {}
for _b, _d, _ns in (("colf", f32, ("kc", "kx", "w2c", "p32", "p4", "limf", "top", "mets")), ("coli", i32, ("pi", "pk", "meti", "mete"))):
    SCRATCH[_b] = ("sbuf", [128, len(_ns)], _d)
    for _i, _n in enumerate(_ns):
        COLS[_n] = (_b, _i)
for _t in range(4):
    SCRATCH["F%d" % _t] = ("sbuf", [128, 256], f16)
    SCRATCH["Z%d" % _t] = ("sbuf", [128, 256], bf)
    SCRATCH["Zo%d" % _t] = ("sbuf", [128, 256], bf)
    for _n, _d in (("UH", f16), ("OP", f16), ("FI", i32), ("FO", f16), ("Fm", f16)):
        SCRATCH["%s%d" % (_n, _t)] = ("sbuf", [128, 128 >> _t, 2, 1 << _t], _d)
BANKS = ["pU", "pR", "pS", "pN", "pA", "pB", "p1", "p2"]
for _n in BANKS:
    SCRATCH[_n] = ("psum", [128, 512], f32)
SEMAPHORES = ["sg", "sv", "ss", "st", "loc"] + ["d%d" % i for i in range(5)] + ["o%s%d" % (c, h) for c in "FZ" for h in range(len(GR))] + \
    ["r%s%d%d" % (c, t, h) for c in "FZ" for t in (1, 2, 3) for h in range(len(GR))]

CYC, TCYC, GATH, WAKE, WIRE = 1.04e-3, 0.52e-3, 1.56, 0.22, 3.0


def rank_program(g, core, T, topo):
    rank = T.rank_of(core)
    if rank is None:
        return
    nrank = len(T.cores)
    eng = {"g": g, "v": g.vector, "s": g.scalar, "t": g.tensor, "y": g.sync}
    semof = {"g": "sg", "v": "sv", "s": "ss", "t": "st"}
    ops = []
    hist = {}

    def op(q, fn, outs, ins, cost=0.1, sem=None, inc=1):
        me, deps = len(ops), {}
        for accs, wr in ((ins, False), (outs, True)):
            for acc in accs:
                for w, lo, hi, i in hist.get(acc[1], ()):
                    own = ops[i][0] == q
                    if acc[1] in BANKS:
                        if not own or (acc[2] < hi and lo < acc[3] and (w or wr)):
                            deps[i] = deps.get(i, False) or not own
                    elif acc[2] < hi and lo < acc[3] and (w or wr):
                        deps[i] = deps.get(i, False) or w or not own
        ops.append([q, fn, cost, deps, sem or semof[q], inc])
        for accs, wr in ((ins, False), (outs, True)):
            for acc in accs:
                mark(acc[1], acc[2], acc[3], wr, me)
        return me

    def mark(name, lo, hi, wr, me):
        h = hist.setdefault(name, [])
        if wr and name not in BANKS:
            h[:] = [a for a in h if not (lo <= a[1] and a[2] <= hi)]
        elif wr:
            h[:] = [a for a in h if not (lo <= a[1] and a[2] <= hi and ops[a[3]][0] == ops[me][0])]
        h.append((wr, lo, hi, me))

    def v(name, lo=0, hi=None, st=1, r=128):
        if name in COLS:
            name, lo = COLS[name]
            hi = lo + 1
        hi = SCRATCH[name][1][1] if hi is None else hi
        ap = T[name][0:r, lo:hi:st] if st > 1 else T[name][0:r, lo:hi]
        return (ap, name, lo, hi, (hi - lo + st - 1) // st)

    def v4(base, t, a, b, which=None):
        name, w = "%s%d" % (base, t), 2 << t
        ap = T[name][:, a // w:b // w, :, :] if which is None else T[name][:, a // w:b // w, which, :]
        return (ap, name, a, b, b - a if which is None else (b - a) // 2)

    def vcost(o, *ins):
        two = all(x[1] not in BANKS and SCRATCH[x[1]][2] in (bf, f16, u16) for x in (o,) + ins[:1])
        if len(ins) == 2:
            return max(64, o[4] * (1 if ins[0][1] in BANKS or ins[1][1] in BANKS else 2)) * CYC
        return max(64, o[4] * (0.5 if two else 1)) * CYC

    def tt(o, a, b, f):
        op("v", lambda: g.vector.tensor_tensor(o[0], a[0], b[0], f), [o], [a, b], vcost(o, a, b))

    def ts(o, a, s1, f1, s2=None, f2=None):
        ins = [a] + [s for s in (s1, s2) if isinstance(s, tuple)]
        x1 = s1[0] if isinstance(s1, tuple) else s1
        x2 = s2[0] if isinstance(s2, tuple) else s2
        if f2 is None:
            op("v", lambda: g.vector.tensor_scalar(o[0], a[0], x1, None, f1), [o], ins, vcost(o, a))
        else:
            op("v", lambda: g.vector.tensor_scalar(o[0], a[0], x1, x2, f1, f2), [o], ins, vcost(o, a))

    def cp(o, a):
        op("v", lambda: g.vector.tensor_copy(o[0], a[0]), [o], [a], vcost(o, a))

    def fill(o, c):
        op("v", lambda: g.vector.memset(o[0], c), [o], [])

    def red(o, a):
        op("v", lambda: g.vector.tensor_reduce(o[0], a[0], AxisListType.X, Op.add), [o], [a])

    def mm(o, l, r, start, stop):
        me = op("t", lambda: g.tensor.matmul(o[0], l[0], r[0], start, stop), [o], [l, r], max(64, r[4]) * TCYC)
        if start and o[1] in closed:
            ops[me][3].setdefault(closed[o[1]], False)
        if stop:
            closed[o[1]] = me

    def act(o, a, func, **kw):
        op("s", lambda: g.scalar.activation(o[0], a[0], func, **kw), [o], [a], max(64, o[4]) * CYC)

    def asel(o, a, pat, cop, base, cm):
        op("g", lambda: g.affine_select(o[0], a[0], pat, cop, 0.0, base, cm), [o], [a], 0.17 + 2 * o[4] * CYC)

    def iota(o, pat, base, cm, small=True):
        if small:
            op("g", lambda: g.iota(o[0], pat, base, cm, allow_small_or_imprecise_dtypes=True), [o], [])
        else:
            op("g", lambda: g.iota(o[0], pat, base, cm), [o], [])

    def mat(name, k):
        return v(name, 128 * k, 128 * k + 128)

    lists, closed = {}, {}
    X = (T.X[:, 0:2048], "X", 0, 2048)

    op("y", lambda: g.sync.dma_start(T.Z0[:], T.vein[:]), [v("Z0")], [], 2.0, "d0", 16)
    op("y", lambda: g.sync.dma_start(T.win[:], T.w[:]), [v("win")], [], 2.0, "d1", 16)
    op("y", lambda: g.sync.dma_start(T.fin[:], T.front[:]), [v("fin")], [], 2.0, "d2", 16)
    op("y", lambda: g.sync.dma_start(T.X[:, 0:2048], T.rock[:]), [X], [], 2.0, "d3", 16)
    op("y", lambda: g.sync.dma_start(T.lin[:], T.lim[:]), [v("lin")], [], 2.0, "d4", 16)

    fill(v("one"), 1.0)
    iota(v("pi"), [[0, 1]], 0, 1, False)
    asel(v("BD1"), v("one", 0, 128), [[-16, 8], [0, 16]], Op.is_ge, 0, 1)
    asel(v("BD"), v("BD1"), [[16, 8], [0, 16]], Op.is_ge, 15, -1)
    asel(v("I"), v("one", 0, 128), [[-1, 128]], Op.is_equal, 0, 1)
    iota(v("RC", r=2), [[0, 8], [37, 16]], 0, 0)
    for m in range(5):
        fill(v("RM", 96 * m, 96 * m + 96, r=2), float(32 << m))
        fill(v("RM", 96 * m, 96 * m + 96, r=1), float(m * (32 << m)))
    fill(v("RC", r=1), 613.0)
    ts(v("pk"), v("pi"), 15, Op.bitwise_and)
    cp(v("kc"), v("pk"))
    cp(v("F0"), v("fin"))
    ts(v("w2c"), v("win"), 2.0, Op.mult)
    ts(v("W2"), v("BD"), v("w2c"), Op.mult)
    for m in range(5):
        act(mat("I5", m), v("I"), Act.Copy, scale=float(32 << m))

    def prep(t, ch):
        kind, a, b = ch
        n = b - a
        F, Z = v("F%d" % t, a, b), v("Z%d" % t, a, b)
        mm(v("pU", 0, n), v("W2"), Z, True, False)
        mm(v("pU", 0, n), v("one", 0, 128, r=1), v("one", 0, n, r=1), False, True)
        mm(v("pU", n, 2 * n), v("BD"), Z, True, True)
        mm(v("pU", 2 * n, 3 * n), v("I"), F, True, True)
        for m in range(5):
            o = v("pR", m * n, m * n + n)
            mm(o, v("RC", r=2), v("RM", 96 * m, 96 * m + n, r=2), True, False)
            mm(o, mat("I5", m), F, False, True)
        cp(v("usi", 2 * a, 2 * b), v("pU", 0, 2 * n))
        ts(v("u2", a, b), v("usi", 2 * a, 2 * a + n), 4095, Op.bitwise_and)
        tt(v("P", a, b), v("pU", 2 * n, 3 * n), v("u2", a, b), Op.mult)
        for m in range(5):
            cm = (5 * a + m * n, 5 * a + m * n + n)
            tt(v("Q", *cm), v("pR", m * n, m * n + n), v("P", a, b), Op.add)
            ts(v("C", *cm), v("Q", *cm), 5 + m, Op.logical_shift_right, 2047, Op.bitwise_and)
            if kind == "S":
                cp(v("off6", 6 * a + m, 6 * b - 5 + m, 6), v("C", *cm))
        if kind == "V":
            cp(v("offV", 0, 5 * n), v("C", 5 * a, 5 * b))
        cp(v("c16", 5 * a, 5 * b), v("C", 5 * a, 5 * b))
        ts(v("si", a, b), v("usi", 2 * a + n, 2 * b), 15, Op.bitwise_and)
        ts(v4("OP", t, a, b), v("si", a, b), v("kc"), Op.is_equal)
        ts(v4("UH", t, a, b), v("u2", a, b), 0.5, Op.mult, -0.5, Op.add)
        ts(v("zq", a, b), Z, 0.25, Op.mult, 1279.625, Op.add)
        ts(v("Kn", a, b), F, float(KN), Op.add)

    def spread(t, ch):
        kind, a, b = ch
        for k in range(16):
            asel(v("Zx", k, 16 * (b - a) - 15 + k, 16), v("Z%d" % t, a, b), [[0, b - a]], Op.is_gt, 1, 0)

    def gather_s(t, ch):
        for i in range(ch[1], ch[2]):
            def one(o, f, z):
                op("s", lambda: g.scalar.activation(o[0], X[0].indirect(f[0]), Act.Abs, bias=z[0], scale=-1.0), [o], [X, f, z], 0.065 + 80 * GATH * CYC)
            one(v("A", 80 * i, 80 * i + 80), v("off6", 6 * i, 6 * i + 5), v("Z%d" % t, i, i + 1))

    def gather_v(t, ch):
        n = ch[2] - ch[1]
        for m in range(5):
            def one(o, f, z):
                op("v", lambda: g.vector.tensor_tensor(o[0], X[0].indirect(f[0]), z[0], Op.subtract), [o], [X, f, z], 0.05 + o[4] * GATH * CYC)
            one(v("D", 16 * n * m, 16 * n * (m + 1)), v("offV", m * n, m * n + n), v("Zx", 0, 16 * n))

    def abs_v(ch):
        n, a = ch[2] - ch[1], 80 * ch[1]
        for m in range(5):
            act(v("A", a + 16 * n * m, a + 16 * n * (m + 1)), v("D", 16 * n * m, 16 * n * (m + 1)), Act.Abs)

    def view5(name, kind, n, m, off=0):
        if kind == "S":
            return v(name, off + m, off + 5 * n - 4 + m, 5)
        return v(name, off + m * n, off + m * n + n)

    def score(ch):
        kind, a, b = ch
        n = b - a
        step = SUB if kind == "S" else n
        mm(v("pS", 0, 5 * n), v("KC", r=2), v("MCS" if kind == "S" else "MCV", 0, 5 * n, r=2), True, False)
        for m in range(5):
            mm(view5("pS", kind, n, m), v("I"), v("c16", 5 * a + m * n, 5 * a + m * n + n), False, False)
        for p in range(a, b, step):
            w, off = step, 5 * (p - a)
            o, on = v("pS", off, off + 5 * w), v("pN", off, off + 5 * w)
            for k in range(16):
                mm(o, mat("ES", k), v("A", 80 * p + k, 80 * (p + w) - 15 + k, 16), False, k == 15 and p + w == b)
            pieces = 1 if kind == "S" else 5
            for c in range(pieces):
                x = (80 * p + c * 80 * w // pieces, 80 * p + (c + 1) * 80 * w // pieces)
                ts(v("NR", *x), v("A", *x), v("top"), Op.is_le)
            for k in range(16):
                mm(on, mat("E", k), v("NR", 80 * p + k, 80 * (p + w) - 15 + k, 16), k == 0, k == 15)

    def choose(t, ch):
        kind, a, b = ch
        n = b - a
        KB = v("KB", a, b)
        K1, K2 = v("K1", a, b), v("K2", a, b)
        tt(K1, view5("pS", kind, n, 0), v("Kn", a, b), Op.min)
        tt(K2, view5("pS", kind, n, 1), v("Kn", a, b), Op.min)
        tt(K1, view5("pS", kind, n, 2), K1, Op.min)
        tt(K2, view5("pS", kind, n, 3), K2, Op.min)
        tt(K1, view5("pS", kind, n, 4), K1, Op.min)
        tt(KB, K1, K2, Op.min)
        for m in range(5):
            tt(view5("EQm", kind, n, m, 5 * a), view5("pS", kind, n, m), KB, Op.is_equal)
        tt(v("TT", 5 * a, 5 * b), v("EQm", 5 * a, 5 * b), v("pN", 0, 5 * n), Op.mult)
        cnt = v("pN", 416, 416 + n)
        for m in range(5):
            mm(cnt, v("I25"), view5("TT", kind, n, m, 5 * a), m == 0, False)
        mm(cnt, v("c85", r=1), v("one", 0, n, r=1), False, True)
        tt(v("KF", a, b), cnt, KB, Op.max)
        tt(v("KI", a, b), v("KF", a, b), v("Kn", a, b), Op.min)
        ts(v4("FI", t, a, b), v("KI", a, b), 2047, Op.bitwise_and)

    def meeting(t, gi):
        a, b = GR[gi]
        h = (b - a) // 2
        q0, q1 = a // 2, b // 2
        per = max(x for x in (1, 2, 4, 8, 16) if x * h <= 512)
        rounds = [(r, "pA" if (r // per) % 2 == 0 else "pB") for r in range(0, 16, per)]
        S, J = v("SJ", a, a + h), v("SJ", a + h, b)

        def pr(name):
            for buf, names in (("ph", ("nv", "nvS", "t1", "t2", "ohS", "ohJ")), ("pb", ("mj", "w0", "wM", "ms"))):
                if name in names:
                    return v(buf, 128 * names.index(name) + q0, 128 * names.index(name) + q1)
            return v(name, q0, q1)

        def big(name, k, c=1):
            return v(name, 8 * a + k * h, 8 * a + (k + c) * h)
        G, LM, XP, SN = (v("p1", 112 * i, 112 * i + h) for i in range(4))
        HF = v("pN", 416, 416 + h)
        ML, MT, JN = (v("p2", 112 * i, 112 * i + h) for i in range(3))
        ts(v("Hh", a, a + h), v4("FI", t, a, b, 0), 0.125, Op.mult, 1279.5625, Op.add)
        ts(v("Hh", a + h, b), v4("FI", t, a, b, 1), 0.125, Op.mult, 1279.5625, Op.add)
        cp(S, v4("FI", t, a, b, 0))
        cp(J, v4("FI", t, a, b, 1))
        for r, bank in rounds:
            for l in range(per):
                o = v(bank, l * h, l * h + h)
                mm(o, mat("B", r + l), v("Hh", a, a + h), True, True)
            for l in range(per):
                tt(big("EQ2", r + l), v(bank, l * h, l * h + h), v("Hh", a + h, b), Op.is_equal)
        for l in range(16):
            mm(HF, v("LT"), big("EQ2", l), l == 0, l == 15)
        for l in range(16):
            mm(ML, mat("Q4", l), big("EQ2", l), l == 0, l == 15)
        for l in range(16):
            mm(G, v("W32"), big("EQ2", l), l == 0, l == 15)
        cp(pr("ohS"), v4("OP", t, a, b, 0))
        cp(pr("ohJ"), v4("OP", t, a, b, 1))
        tt(pr("JS"), J, S, Op.mult)
        jq = v("pU", 320, 320 + h)
        mm(jq, v("I32"), J, True, False)
        mm(jq, v("I32"), v4("UH", t, a, b, 1), False, True)
        tt(pr("JQ"), jq, pr("JS"), Op.add)
        ts(pr("Jn"), pr("JQ"), 5, Op.logical_shift_right, 2047, Op.bitwise_and)
        tt(pr("t1"), pr("Jn"), J, Op.subtract)
        ts(pr("w0"), HF, 0.0, Op.is_gt)
        tt(pr("wM"), ML, pr("w0"), Op.mult)
        ts(pr("mj"), G, v("p32"), Op.is_ge)
        mm(LM, v("BD"), pr("wM"), True, True)
        ts(pr("ms"), LM, v("p4"), Op.is_ge)
        mm(XP, v("BM"), pr("ms"), True, False)
        mm(XP, v("BN"), pr("mj"), False, True)
        for r, bank in rounds:
            for k in range(per):
                mm(v(bank, k * h, k * h + h), mat("B", r + k), J, True, True)
            for k in range(per):
                ts(big("MK", r + k), XP, v("KX", r + k, r + k + 1), Op.is_equal)
            tt(big("PJ", r, per), v(bank, 0, per * h), big("MK", r, per), Op.mult)
        ts(pr("nv"), XP, v("KX", 15, 16), Op.is_gt)
        tt(pr("nvS"), pr("nv"), S, Op.mult)
        mm(SN, v("I"), pr("nvS"), True, False)
        for k in range(16):
            mm(SN, v("I"), big("PJ", k), False, k == 15)
        tt(pr("t2"), pr("t1"), pr("mj"), Op.mult)
        mm(JN, v("I"), J, True, False)
        mm(JN, v("I"), pr("t2"), False, True)
        mm(MT, v("S15"), pr("mj"), True, True)
        tt(v4("Fm", t, a, b, 1), JN, pr("ohJ"), Op.mult)
        tt(v4("Fm", t, a, b, 0), SN, pr("ohS"), Op.mult)
        cp(v4("FO", t, a, b, 1), JN)
        cp(v4("FO", t, a, b, 0), SN)
        red(v("metc", gi, gi + 1), MT)

    def send(t, gi, what, src):
        dst = T.cores[(rank + NEXT) % nrank]
        rid, pid = topo.addr(dst, core)
        es = topo.engines(core, dst)[:8]
        a, b = GR[gi]
        sem = "r%s%d%d" % (what, t + 1, gi)

        def call():
            g.remote_dma(out_ap=T["%s%d" % (what, t + 1)][:, a:b], in_ap=src[0], remote_sem=T.sem[sem], local_sem=T.sem["loc"],
                         pid=pid, routing_id=rid, dma_engine_mask=sum(1 << e for e in es))
        me = op("g", call, [], [src], 0.4, "loc", len(es))
        ops.append(["r", None, WIRE, {me: False}, sem, len(topo.engines(T.cores[(rank - NEXT) % nrank], core)[:8])])
        mark("%s%d" % (what, t + 1), a, b, True, len(ops) - 1)

    def mining(t, gi):
        a, b = GR[gi]
        n, c0, c1 = b - a, a // 16, b // 16
        FO, Z, o, f = v4("FO", t, a, b), v("Z%d" % t, a, b), v("Y", a, b), v("Ol", c0, c1)
        OL, ER, VN, CN, LL = v("p2", 448, 448 + n // 16), v("pA", 0, n), v("pB", 0, n), v("pA", 256, 256 + n), v("p2", 480, 480 + n // 16)
        if t < 3:
            send(t, gi, "F", FO)
        else:
            cp(v("yo", a, b), FO)
            op("y", lambda: g.sync.dma_start(T.yf[:, a:b], T.yo[:, a:b]), [], [v("yo", a, b)], 2.0, "oF%d" % gi, 16)
        w = 2 << t
        for q in range(16):
            col = (T["Fm%d" % t][:, a // w + q // w:b // w:16 // w, q % w // (w // 2), q % (w // 2)], "Fm%d" % t, a, b, n // 16)
            mm(OL, mat("E", q), col, q == 0, q == 15)
        mm(ER, v("BD"), v4("Fm", t, a, b), True, True)
        cp(f, OL)
        cp(v("Ouf", c0, c1), OL)
        cp(v("Er", a, b), ER)
        op("s", lambda: g.scalar.activation(o[0], X[0].indirect(f[0]), Act.Copy), [o], [X, f], 0.065 + n * GATH * CYC)
        if gi == len(GR) - 1:
            for x in range(gi):
                scatter(x)
        mm(VN, v("Ihalf"), Z, True, False)
        mm(VN, v("q9"), v("one", 0, n), False, False)
        mm(VN, v("Ihalf"), o, False, True)
        ts(v("zt", a, b), VN, 1280.0, Op.add)
        ts(v("Zo%d" % t, a, b), v("zt", a, b), -1280.0, Op.add)
        if t < 3:
            send(t, gi, "Z", v("Zo%d" % t, a, b))
        else:
            op("y", lambda: g.sync.dma_start(T.yz[:, a:b], T["Zo3"][:, a:b]), [], [v("Zo3", a, b)], 2.0, "oZ%d" % gi, 16)

        def later(c):
            lo = max(16 * c, a)
            w = (T.EQW[:, c, lo - 16 * c:b - 16 * c], "EQW", 256 * c + lo - 16 * c, 256 * c + b - 16 * c, b - lo)
            return lo, w
        for c in range(c1):
            lo, w = later(c)
            ts(w, v("Er", lo, b), v("Ouf", c, c + 1), Op.is_equal)
        dg = (T.EQW[:, c0:c1, 0:16], "EQW", 256 * c0, 256 * c1, n)
        op("v", lambda: g.vector.tensor_tensor(dg[0], dg[0], T.DM[:, c0:c1, :], Op.mult), [dg], [dg, ("", "DM", 0, 256)], 2 * n * CYC)
        for c in range(c1):
            lo, w = later(c)
            mm(v("pA", 256 + lo - a, 256 + n), v("BD"), w, c == 0, c == c1 - 1)
        act(v("lo", a, b), CN, Act.Sign)
        mm(LL, v("I"), v("IO", c0, c1), True, False)
        mm(LL, v("c16k", r=1), v("one", 0, n // 16, r=1), False, False)
        for q in range(16):
            mm(LL, mat("ES", q), v("lo", a + q, b - 15 + q, 16), False, q == 15)
        tt(v("R1", a, b), o, v("zq", a, b), Op.subtract)
        ts(v("R2", a, b), v("R1", a, b), 1280.0, Op.add, 0.0, Op.max)
        tt(v("LO", c0, c1), LL, v("Ouf", c0, c1), Op.max)
        cp(v("Ls", c0, c1), v("LO", c0, c1))
        lists[gi] = (v("Ls", c0, c1), v("R2", a, b))

    def scatter(gi):
        XW, ls, r2 = (T.X[:, 0:2560], "X", 0, 2560), lists[gi][0], lists[gi][1]
        op("v", lambda: g.vector.tensor_copy(XW[0].indirect(ls[0]), r2[0]), [XW], [ls, r2], 0.05 + r2[4] * 3.8 * CYC)

    def limits(t):
        if t == 0:
            cp(v("limf"), v("lin"))
            cp(v("top"), v("limf"))
        else:
            red(v("mets"), v("metc", 0, len(GR)))
            cp(v("meti"), v("mets"))
            ts(v("mete"), v("meti"), 3, Op.bitwise_and)
            tt(v("top"), v("limf"), v("mete"), Op.add)

    def key_constants():
        for k in range(16):
            asel(mat("E", k), v("BD"), [[0, 8], [1, 16]], Op.is_equal, -k, 0)
            act(mat("ES", k), mat("E", k), Act.Copy, scale=10240.0)
        iota(v("KC", r=2), [[0, 128]], -4096, 6144)
        iota(v("MCS", r=2), [[0, 96], [1, 5]], 0, 0)
        iota(v("MCV", 0, 5 * NV, r=2), [[1, 5], [0, NV]], 0, 0)
        fill(v("MCS", r=1), 4096.0)
        fill(v("MCV", 0, 5 * NV, r=1), 4096.0)

    def last_constants():
        iota(v("io"), [[1, 16]], 0, 0)
        op("g", lambda: g.iota(T.DMi[:], [[0, 16], [1, 16]], 0, 0, allow_small_or_imprecise_dtypes=True), [("", "DMi", 0, 256)], [])
        act(v("I25"), v("I"), Act.Copy, scale=-float(1 << 25))
        fill(v("c85"), 8.5 * (1 << 25))
        fill(v("c16k"), -163840.0)
        ts(v("I32"), v("I"), 32.0, Op.mult)
        ts(v("Ihalf"), v("I"), 0.5, Op.mult)
        fill(v("q9"), -(2.0 ** -9))
        ts(v("OH"), v("io"), v("kc"), Op.is_equal)
        for l in range(16):
            ts(mat("B", l), v("BD"), v("OH", l, l + 1), Op.mult)
            act(mat("Q4", l), v("I"), Act.Copy, scale=float(4 ** (15 - l)))
        for r in range(16):
            fill(v("PW", r, r + 1), 2.0 ** (5 * (15 - r)))
            fill(v("PW", 16 + r, 17 + r), 2.0 ** (2 * (16 - r)))
        for j, name in ((0, "p32"), (16, "p4")):
            tt(v("PT", j, j + 16), v("PW", j, j + 16), v("OH"), Op.mult)
            red(v(name), v("PT", j, j + 16))
        asel(v("LT"), v("BD"), [[1, 128]], Op.is_gt, 0, -1)
        ts(v("LT"), v("LT"), -32.0, Op.mult)
        tt(v("LT"), v("LT"), v("I"), Op.add)
        ts(v("W32"), v("BD"), v("p32"), Op.mult)
        ts(v("BN"), v("BD"), -1.0, Op.mult)
        ts(v("BD1"), v("I"), -64.0, Op.mult)
        tt(v("BM"), v("BD1"), v("BD"), Op.add)
        ts(v("S15"), v("one", 0, 128), v("OH", 15, 16), Op.mult)
        ts(v("kx"), v("kc"), 65.0, Op.add)
        ts(v("KX"), v("io"), v("kx"), Op.subtract)
        op("v", lambda: g.vector.tensor_scalar(T.DM[:], T.DMi[:], v("kc")[0], None, Op.is_gt), [("", "DM", 0, 256)], [("", "DMi", 0, 256), v("kc")], 256 * CYC)
        ts(v("PT", 16, 32), v("io"), 32.0, Op.mult, 2048.0, Op.add)
        ts(v("PT", 32, 33), v("kc"), 2.0, Op.mult)
        ts(v("IO"), v("PT", 16, 32), v("PT", 32, 33), Op.add)

    vch = [ch for ch in CH if ch[0] == "V"][0]
    for t in range(4):
        if t == 0:
            for ch in CH:
                prep(0, ch)
            key_constants()
            last_constants()
        else:
            for ch in CH:
                if ch[1] >= GR[-1][0]:
                    prep(t, ch)
        spread(t, vch)
        for ch in CH:
            if ch[0] == "S":
                gather_s(t, ch)
        gather_v(t, vch)
        limits(t)
        abs_v(vch)
        for gi, (a, b) in enumerate(GR):
            for ch in CH:
                if a <= ch[1] < b:
                    score(ch)
                    choose(t, ch)
            meeting(t, gi)
            mining(t, gi)
            if gi == len(GR) - 1:
                scatter(gi)
            elif t < 3:
                for ch in CH:
                    if a <= ch[1] < b:
                        prep(t + 1, ch)
    op("y", lambda: g.sync.dma_start(T.yx[:], T.X[:, 0:2048]), [], [X], 2.0, "d3", 16)

    succ = [[] for _ in ops]
    left = [0] * len(ops)
    for i, o in enumerate(ops):
        for j in o[3]:
            succ[j].append(i)
            left[i] += 1
    way = [0.0] * len(ops)
    for i in range(len(ops) - 1, -1, -1):
        best = 0.0
        for j in succ[i]:
            best = max(best, way[j] + (WAKE if ops[j][3][i] else 0.0))
        way[i] = best + ops[i][2]
    free, ready = {}, {}
    early = [0.0] * len(ops)
    for i, o in enumerate(ops):
        free[o[0]] = 0.0
        ready.setdefault(o[0], [])
        if not left[i]:
            ready[o[0]].append(i)
    order = []
    while len(order) < len(ops):
        pick = None
        for q, r in ready.items():
            if r:
                start = max(free[q], min(early[i] for i in r))
                if pick is None or start < pick[0]:
                    pick = (start, q)
        start, q = pick
        i = max((i for i in ready[q] if early[i] <= start + 1e-9), key=lambda i: way[i])
        ready[q].remove(i)
        end = start + ops[i][2]
        if q != "r":
            free[q] = end if q != "y" else start + 0.1
        order.append(i)
        for j in succ[i]:
            left[j] -= 1
            early[j] = max(early[j], end + WAKE if ops[j][3][i] else (end if ops[j][0] == "r" else start))
            if not left[j]:
                ready[ops[j][0]].append(j)

    count, know, value, clocks = {}, {q: {} for q in free}, {}, {}
    for i in order:
        q, fn, cost, deps, sem, inc = ops[i]
        k = know[q]
        best = {}
        for j, wait in deps.items():
            if wait and (ops[j][4] not in best or value[best[ops[j][4]]] < value[j]):
                best[ops[j][4]] = j
        for j in sorted(best.values(), key=lambda j: -len(clocks[j])):
            if k.get(ops[j][4], 0) < value[j]:
                eng[q].wait_ge(T.sem[ops[j][4]], value[j])
                for s, x in clocks[j].items():
                    if k.get(s, 0) < x:
                        k[s] = x
        count[sem] = value[i] = count.get(sem, 0) + inc
        clocks[i] = {sem: value[i]}
        if q != "r":
            r = fn()
            if r is not None:
                r.then_inc(T.sem[sem], inc)
            clocks[i] = dict(k)
            clocks[i][sem] = value[i]
    for s in SEMAPHORES:
        if count.get(s):
            g.wait_ge(T.sem[s], count[s])
